import numpy as np, ml_dtypes
CORES = [16,17,18,19,32,33,34,35]
N = 8
import mx_ref
BF = ml_dtypes.bfloat16
def pick(q, e):
    c = np.concatenate([q[0].reshape(128, -1, 4), np.zeros((128, 1, 4), np.uint8)], axis=1); s = np.concatenate([q[1], np.ones((16, 1), np.uint8)], axis=1)
    return (np.ascontiguousarray(c[:, e].reshape(128, -1)), np.ascontiguousarray(s[:, e]))
def join(*qs):
    return (np.concatenate([q[0] for q in qs], axis=1), np.concatenate([q[1] for q in qs], axis=1))
def put(q, e, v):
    c, s = q[0].reshape(128, -1, 4).copy(), q[1].copy(); c[:, e] = v[0].reshape(128, -1, 4); s[:, e] = v[1]
    return (c.reshape(128, -1), s)
def pk(c, s):
    return (np.ascontiguousarray(c), mx_ref.live(s))
def emit(q):
    return q[0], q[1]
def decode(q):
    o = []
    for b in range(4):
        e = np.zeros((128, 128, 4), np.float32); e[np.arange(128), np.arange(128), b] = 1
        o.append(mx_ref.matmul(mx_ref.quantize(e.reshape(128, 512).astype(BF)), q))
    return np.stack(o, axis=2).reshape(128, -1)
def f(rng, *shape):
    return mx_ref.flush((rng.standard_normal(shape, dtype=np.float32) * np.exp2(rng.integers(-2, 3, shape[:-1] + (1,)))).astype(BF))
def wide(rng, *shape, cols=0):
    v = rng.standard_normal(shape, dtype=np.float32) * np.exp2(rng.integers(-12, 13, shape)).astype(np.float32)
    if cols: v *= np.repeat(np.exp2(rng.integers(-cols, cols + 1, shape[:-2] + (1, shape[-1] // 4))) * (rng.random(shape[:-2] + (1, shape[-1] // 4)) > 0.0625), 4, axis=-1).astype(np.float32)
    return mx_ref.flush(v.astype(BF))
P, K, R = 128, 32, 3
def lift(v):
    v = np.asarray(v).astype(np.float32)
    v[np.abs(v) < np.float32(2.0 ** -16)] = 0
    return v.astype(BF)
def whole(x, hc, u, w):
    i = np.arange(N)
    return {"x": x, "hl": hc[(i - 1) % N], "hc": hc, "hr": hc[(i + 1) % N], "u": u, "w": w}
def query(rng):
    v = np.zeros((N, 128, 512), BF)
    v[:, :, :4] = f(rng, 128, 4)
    return v
def near(rng, hc):
    k = np.repeat(np.exp2(rng.integers(-3, 2, (N, 1, P))), 4, axis=2)
    return lift(hc.astype(np.float32) + f(rng, N, 128, 4 * P).astype(np.float32) * k)
def setup_inputs(rng):
    hc = lift(f(rng, N, 128, 4 * P))
    return whole(near(rng, hc), hc, query(rng), f(rng, N, 128, 512))
def setup_inputs_spread(rng):
    hc = lift(wide(rng, N, 128, 4 * P, cols=4))
    return whole(lift(wide(rng, N, 128, 4 * P, cols=4)), hc, query(rng), f(rng, N, 128, 512))
def setup_inputs_ties(rng):
    d = setup_inputs(rng)
    g = rng.permutation(P) // 7
    s = np.repeat(1 - 2 * rng.integers(0, 2, P), 4).astype(np.float32)
    def same(v):
        return (v.reshape(N, 128, P, 4)[:, :, g].reshape(N, 128, 4 * P).astype(np.float32) * s).astype(BF)
    return whole(same(d["x"]), same(d["hc"]), d["u"], d["w"])
def setup_inputs_again(rng):
    d = setup_inputs(rng)
    k = np.ones(P, np.float32)
    k[rng.permutation(P)[:K]] = 1024
    k = np.repeat(k, 4)
    return whole(lift(d["x"].astype(np.float32) * k), lift(d["hc"].astype(np.float32) * k), d["u"], d["w"])
def setup_inputs_still(rng):
    d = setup_inputs(rng)
    v = rng.integers(128, 256, (16, 8, P, 4)) * np.exp2(rng.integers(-10, -7, (16, 8, P, 4)))
    v[:, 0, :, 0] = (128 + 8 * np.argsort(rng.random((16, P)), axis=0) + rng.integers(1, 8, (16, P))) * 2.0 ** -7
    v = v * rng.choice([-1.0, 1.0], v.shape) * np.exp2(rng.integers(-2, 3, (16, 1, P, 1)))
    v = v.reshape(128, 4 * P).astype(np.float32).astype(BF)
    held = decode(mx_ref.quantize(v)).astype(BF)
    s = int(rng.integers(0, N))
    hc = np.array(d["hc"])
    for r in range(s - 1, s + 3): hc[r % N] = v
    x = near(rng, hc)
    x[s] = held
    few = np.array(x[(s + 1) % N]).reshape(128, P, 4)
    rest = rng.permutation(P)[K // 2:]
    few[:, rest] = held.reshape(128, P, 4)[:, rest]
    x[(s + 1) % N] = few.reshape(128, 4 * P)
    return whole(x, hc, d["u"], d["w"])
def setup_inputs_one(rng):
    d = setup_inputs(rng)
    p, t = int(rng.integers(0, 128)), int(rng.integers(0, 4))
    u = np.zeros((N, 128, 512), BF)
    u[:, p, t] = -1.5
    off = np.sort(rng.permutation(P)[K // 2:])
    x, hc = np.array(d["x"]).reshape(N, 128, P, 4), np.array(d["hc"]).reshape(N, 128, P, 4)
    x[:, :, off[::2]] = (x[:, :, off[::2]].astype(np.float32) - np.float32(128)).astype(BF)
    x[:, p, off, t] = 0
    hc[:, p, off, t] = 0
    return whole(x.reshape(N, 128, 4 * P), hc.reshape(N, 128, 4 * P), u, d["w"])
def check_inputs(d):
    b = []
    for k, lo, hi in (("x", -16, 24), ("hl", -16, 24), ("hc", -16, 24), ("hr", -16, 24), ("u", -30, 30), ("w", -30, 30)):
        v = np.abs(d[k].astype(np.float32))
        if not (np.isfinite(v).all() and ((v == 0) | (v >= 2.0 ** lo) & (v <= 2.0 ** hi)).all()): b.append("a value of " + k)
    i = np.arange(N)
    hl, hc, hr, u = [d[k].astype(np.float32) for k in ("hl", "hc", "hr", "u")]
    if (hl != hc[(i - 1) % N]).any(): b.append("hl isn't the left neighbour's hc")
    if (hr != hc[(i + 1) % N]).any(): b.append("hr isn't the right neighbour's hc")
    if (u != u[:1]).any(): b.append("u isn't the same on all ranks")
    if (d["u"][:, :, 4:].astype(np.float32) != 0).any(): b.append("u has numbers behind its column 0")
    return b
def reference(x, hl, hc, hr, u, w):
    a, h, b = [[mx_ref.quantize(np.ascontiguousarray(v[r])) for r in range(N)] for v in (hl, hc, hr)]
    s = [x[r] for r in range(N)]
    ch = np.zeros((N, R, K), np.float32)
    for t in range(R):
        dh = decode(join(*h)).reshape(128, N, 4 * P).transpose(1, 0, 2)
        at, dq = [], []
        for r in range(N):
            v = ((dh[(r - 1) % N] + dh[(r + 1) % N]) - dh[r] * np.float32(2)) * np.float32(0.25)
            s[r] = (s[r].astype(np.float32) + v).astype(BF)
            q = mx_ref.quantize(np.ascontiguousarray((s[r].astype(np.float32) - dh[r]).astype(BF)))
            z = np.abs(mx_ref.matmul(mx_ref.quantize(np.ascontiguousarray(u[r])), q)[0]) + np.float32(0)
            e = np.argsort(-z, kind="stable")[:K]
            ch[r, t] = e
            at.append(e)
            dq.append(pick(q, e))
        dd = decode(join(*dq)).reshape(128, N, K, 4)
        for r in range(N):
            v = mx_ref.quantize(np.ascontiguousarray((dh[r].reshape(128, P, 4)[:, at[r]] + dd[:, r]).reshape(128, -1).astype(BF)))
            for held, o in ((a, (r + 1) % N), (h, r), (b, (r - 1) % N)): held[o] = put(held[o], at[r], v)
    oc, osc = np.zeros((N, 128, 12 * P), np.uint8), np.zeros((N, 16, 3 * P), np.uint8)
    y = np.zeros((N, 128, P), np.float32)
    for r in range(N):
        oc[r], osc[r] = emit(join(a[r], h[r], b[r]))
        y[r] = mx_ref.matmul(mx_ref.quantize(np.ascontiguousarray(w[r])), a[r])
    return {"oc": oc, "osc": osc, "xe": np.stack(s).astype(np.float32), "ch": ch, "y": y}

@@ -1,0 +1,325 @@
+from concourse.bass import DstId, RemoteDMATransfer
+from concourse.mybir import dt, AluOpType as OP, AxisListType, ActivationFunctionType as AF
+
+P, K, R = 128, 32, 3
+NEW, SLOT, XC = 128, 160, 168
+WIN, WINH = 168, 296
+CODE, BF, F32, U8 = "float8_e4m3fn_x4", "bfloat16", "float32", "uint8"
+BIG = 256
+ZW = 520
+
+SCRATCH = {"ps": ("psum", [128, 4096], F32)}
+for _n, _w, _d in (("hlb", 512, BF), ("hcb", 512, BF), ("hrb", 512, BF), ("xs", 512, BF), ("wb", 512, BF), ("ub4", 4, BF),
+                   ("ubt", 512, BF), ("dr", 512, BF), ("pt", 512, BF), ("xt", 4 * 136, BF), ("ones", 128, BF),
+                   ("half", 128, BF), ("idm", 128, BF), ("tri", 128, BF), ("zd", 3 * ZW, BF), ("wc", 4 * 130, BF),
+                   ("kk", 512, BF), ("vj", 128, "int32"), ("vi", 128, "int32"), ("mask16", 128, BF), ("pq", 8, "int32"),
+                   ("pr", 8, "int32"), ("mask8", 8, F32), ("nmask8", 8, F32), ("pc", 1, "int32"), ("lo", 1, "int32"),
+                   ("hi", 1, "int32"), ("lof", 1, F32), ("cb", 8, F32), ("cl", 8, F32), ("absS", 128, F32),
+                   ("nac", 1, F32), ("sgn", 128, BF), ("bt", 128, BF), ("rk", 1, F32), ("offE", 2 * R, "uint16"),
+                   ("offL", 24 * R, "uint16"), ("lt", 24 * R, F32), ("ech", 2 * R, F32), ("xef", 512, F32),
+                   ("ysb", 128, F32)):
+    SCRATCH[_n] = ("sbuf", [128, _w], _d)
+for _n, _w in [("e1", 512), ("e25", 512), ("em5", 512), ("wcq", 130), ("uq", 128), ("wq", 128), ("dq", 128), ("fin", 384)] + [
+        ("%s%d" % (_a, _t), _b) for _t in range(R) for _a, _b in (("winA", WIN), ("winB", WIN), ("winH", WINH), ("qp", 128))]:
+    SCRATCH[_n] = ("sbuf", [128, _w], CODE)
+    SCRATCH[_n + "_s"] = ("sbuf", [128, _w], U8)
+
+SEMAPHORES = ["sv", "ss", "sp", "sg", "sent", "sto"] + ["ld" + n for n in ("hl", "hc", "hr", "x", "w", "u")] + [
+    "%s%s%d" % (k, s, t) for k in "cs" for s in "AB" for t in range(R)]
+
+
+def _flow(g, T):
+    eng = {"v": g.vector, "s": g.scalar, "p": g.tensor, "g": g, "y": g.sync}
+    own = {"v": "sv", "s": "ss", "p": "sp", "g": "sg"}
+    known = {q: {} for q in eng}
+    total, clock, lastw, reads = {}, {}, {}, {}
+
+    def wait(q, events):
+        need = {}
+        for s, n in events:
+            if known[q].get(s, 0) < n and need.get(s, 0) < n:
+                need[s] = n
+        for s in sorted(need):
+            if not any(s2 != s and clock[(s2, n2)].get(s, 0) >= need[s] for s2, n2 in need.items()):
+                eng[q].wait_ge(T.sem[s], need[s])
+        for s, n in need.items():
+            for k, c in clock[(s, n)].items():
+                known[q][k] = max(known[q].get(k, 0), c)
+
+    def depend(q, rd, wr):
+        ev = []
+        for k in list(rd) + list(wr):
+            bank = k.startswith("ps")
+            if k in lastw and not (bank and q == "p" and lastw[k][0] == "p"):
+                ev.append(lastw[k][1])
+            if bank or k in wr:
+                ev += [e for q2, e in reads.get(k, ()) if q2 != q or k in wr]
+        wait(q, ev)
+
+    def done(q, who, sem, inc, rd, wr):
+        total[sem] = total.get(sem, 0) + inc
+        event = (sem, total[sem])
+        clock[event] = dict(known[q])
+        clock[event][sem] = total[sem]
+        for k in rd:
+            reads.setdefault(k, []).append((who, event))
+        for k in wr:
+            lastw[k] = (who, event)
+            reads[k] = []
+
+    def op(q, fn, rd, wr):
+        depend(q, rd, wr)
+        fn(eng[q]).then_inc(T.sem[own[q]], 1)
+        done(q, q, own[q], 1, rd, wr)
+
+    def dma(q, out, in_, sem, rd, wr):
+        depend(q, rd, wr)
+        eng[q].dma_start(out, in_).then_inc(T.sem[sem], 16)
+        done(q, "d" + q, sem, 16, rd, wr)
+
+    def lands(key, sem, n):
+        total[sem] = n
+        clock[(sem, n)] = {sem: n}
+        lastw[key] = ("r", (sem, n))
+
+    def finish():
+        for s in sorted(total):
+            if known["g"].get(s, 0) < total[s]:
+                g.wait_ge(T.sem[s], total[s])
+
+    return op, dma, depend, lands, finish
+
+
+def _masks(topo, core, left, right):
+    taken, out = set(), {}
+    for dst in sorted((left, right), key=lambda c: len(topo.engines(core, c))):
+        out[dst] = [k for k in topo.engines(core, dst) if k not in taken][:8]
+        taken.update(out[dst])
+    return out
+
+
+def rank_program(g, core, T, topo):
+    rank = T.rank_of(core)
+    if rank is None:
+        return
+    cores = list(T.cores)
+    n = len(cores)
+    left, right = cores[(rank - 1) % n], cores[(rank + 1) % n]
+    masks = _masks(topo, core, left, right)
+
+    def arrives(src):
+        k = cores.index(src)
+        return len(_masks(topo, src, cores[(k - 1) % n], cores[(k + 1) % n])[core])
+
+    op, dma, depend, lands, finish = _flow(g, T)
+    ps = T["ps"]
+
+    def bank(b, lo=0, hi=128):
+        return ps[:, 512 * b + lo:512 * b + hi]
+
+    def q_mx(name, a, b, tile, rd, wr):
+        op("v", lambda e: e.quantize_mx(T[name][:, a:b], T[name + "_s"][:, a:b], tile), rd, wr)
+
+    def mm(b, ln, la, rn, ra, start, stop, rd):
+        op("p", lambda e: e.matmul_mx(bank(b), T[ln][:, la:la + 128], T[ln + "_s"][:, la:la + 128],
+                                      T[rn][:, ra:ra + 128], T[rn + "_s"][:, ra:ra + 128], start, stop),
+           rd, ["ps%d" % b])
+
+    def act(out, in_, func, rd, wr, **kw):
+        op("s", lambda e: e.activation(out, in_, func, **kw), rd, wr)
+
+    def ts(out, in_, s1, s2, rd, wr, *ops):
+        op("v", lambda e: e.tensor_scalar(out, in_, s1, s2, *ops), rd, wr)
+
+    def tt(out, a, b, o, rd, wr):
+        op("v", lambda e: e.tensor_tensor(out, a, b, o), rd, wr)
+
+    def cp(out, in_, rd, wr):
+        op("v", lambda e: e.tensor_copy(out, in_), rd, wr)
+
+    def fill(ap, c, wr):
+        op("v", lambda e: e.memset(ap, c), [], wr)
+
+    def iota(out, pattern, base, cm, wr, **kw):
+        op("g", lambda e: e.iota(out, pattern, base, cm, **kw), [], wr)
+
+    dma("s", T.hcb[:], T.hc[:], "ldhc", [], ["hcb"])
+    dma("y", T.hlb[:], T.hl[:], "ldhl", [], ["hlb"])
+    dma("s", T.hrb[:], T.hr[:], "ldhr", [], ["hrb"])
+    dma("y", T.xs[:], T.x[:], "ldx", [], ["xs0", "xs1", "xs2", "xs3"])
+    dma("s", T.ub4[:], T.u[:, 0:4], "ldu", [], ["ub4"])
+    dma("y", T.wb[:], T.w[:], "ldw", [], ["wb"])
+
+    small = {"allow_small_or_imprecise_dtypes": True}
+    fill(T.ones[:], 1.0, ["ones"])
+    fill(T.zd[:, 0:ZW], 0.0, ["zd0"])
+    fill(T.half[:], -0.5, ["half"])
+    fill(T.wc[:, 3:512:4], 0.0, ["wcw3"])
+    fill(T.wc[:, 512:520], 0.0, ["wcc"])
+    fill(T.xt[:, 0:32], 0.0, ["xt0", "xt1", "xt2"])
+    op("g", lambda e: e.affine_select(T.idm[:], T.ones[:], [[-1, 128]], OP.is_equal, 0.0, 0, 1), ["ones"], ["idm"])
+    iota(T.vj[:], [[-1, 128]], 128, 1, ["vj"])
+    iota(T.pc[:], [[0, 1]], 0, 1, ["pc"])
+    iota(T.pq[:], [[-16, 8]], 0, 1, ["pq"])
+    iota(T.cb[:], [[16, 8]], -BIG, 0, ["cb"], **small)
+    iota(T.kk[:, 0:64], [[1, 16], [0, 2], [16, 2]], 0, 0, ["kk0"], **small)
+    op("g", lambda e: e.affine_select(T.tri[:], T.half[:], [[-1, 128]], OP.is_gt, 0.5, 0, 1), ["half"], ["tri"])
+    act(T.zd[:, 3:515:4], T.idm[:], AF.Copy, ["idm"], ["zd0"])
+    for f, s in ((1, 0.25), (2, -0.5)):
+        act(T.zd[:, ZW * f:ZW * f + ZW], T.zd[:, 0:ZW], AF.Copy, ["zd0"], ["zd%d" % f], scale=s)
+
+    def decoders(f, name):
+        for b in range(4):
+            q_mx(name, 128 * b, 128 * b + 128, T.zd[:, ZW * f + 3 - b:ZW * f + 515 - b], ["zd%d" % f], ["%s%d" % (name, b)])
+
+    decoders(0, "e1")
+    ts(T.vi[:], T.vj[:], 15, None, ["vj"], ["vi"], OP.bitwise_and)
+    ts(T.pr[:], T.pq[:], 4, None, ["pq"], ["pr"], OP.arith_shift_right)
+    ts(T.lo[:], T.pc[:], 15, None, ["pc"], ["lo"], OP.bitwise_and)
+    ts(T.hi[:], T.pc[:], 112, None, ["pc"], ["hi"], OP.bitwise_and)
+    ts(T.mask16[:], T.vi[:], 0, None, ["vi"], ["mask16"], OP.is_equal)
+    ts(T.mask8[:], T.pr[:], 0, None, ["pr"], ["mask8"], OP.is_equal)
+    cp(T.lof[:], T.lo[:], ["lo"], ["lof"])
+    for c, name in ((0, "lo"), (2, "hi"), (5, "lo"), (7, "hi")):
+        cp(T.wc[:, 512 + c:513 + c], T[name][:], [name], ["wcc"])
+    ts(T.cl[:], T.cb[:], T.lof[:], None, ["cb", "lof"], ["cl"], OP.add)
+    for t, s in ((0, -1.0), (1, 1.0), (2, -float(BIG))):
+        act(T.wc[:, t:512:4], T.mask16[:], AF.Copy, ["mask16"], ["wcw%d" % t], scale=s)
+    act(T.nmask8[:], T.mask8[:], AF.Copy, ["mask8"], ["nmask8"], scale=-1.0)
+    for k, w in ((1, 64), (2, 128), (3, 256)):
+        act(T.kk[:, w:2 * w], T.kk[:, 0:w], AF.Copy, ["kk%d" % j for j in range(k)], ["kk%d" % k])
+    decoders(1, "e25")
+    decoders(2, "em5")
+    q_mx("wcq", 0, 130, T.wc[:], ["wcw0", "wcw1", "wcw2", "wcw3", "wcc"], ["wcq"])
+
+    q_mx("winH0", 0, 128, T.hcb[:], ["hcb"], ["H0", "Hs0"])
+    q_mx("winA0", 0, 128, T.hlb[:], ["hlb"], ["A0", "As0"])
+    q_mx("winB0", 0, 128, T.hrb[:], ["hrb"], ["B0", "Bs0"])
+    for t in range(4):
+        ts(T.ubt[:, t:512:4], T.ones[:], T.ub4[:, t:t + 1], None, ["ones", "ub4"], ["ubt%d" % t], OP.mult)
+    q_mx("uq", 0, 128, T.ubt[:], ["ubt0", "ubt1", "ubt2", "ubt3"], ["uq"])
+
+    order = ["A", "B"]
+    if topo.chip(left) != topo.chip(core) and topo.chip(right) == topo.chip(core):
+        order = ["B", "A"]
+
+    def both(side, t):
+        return ["%s%d" % (side, t), "%ss%d" % (side, t)]
+
+    def state_first(t):
+        for b in range(4):
+            mm(b, "e25", 128 * b, "win%s%d" % (order[0], t), 0, True, False, ["e25%d" % b] + both(order[0], t))
+
+    def state_second(t):
+        for b in range(4):
+            mm(b, "e25", 128 * b, "win%s%d" % (order[1], t), 0, False, False, ["e25%d" % b] + both(order[1], t))
+            mm(b, "em5", 128 * b, "winH%d" % t, 0, False, True, ["em5%d" % b] + both("H", t))
+            xb, db = T.xs[:, b:512:4], T.dr[:, b:512:4]
+            tt(xb, xb, bank(b), OP.add, ["xs%d" % b, "ps%d" % b], ["xs%d" % b])
+            tt(db, xb, bank(4 + b), OP.subtract, ["xs%d" % b, "ps%d" % (4 + b)], ["dr%d" % b])
+
+    def decode_own(t, b, alone):
+        mm(4 + b, "e1", 128 * b, "winH%d" % t, 0, True, alone, ["e1%d" % b] + both("H", t))
+
+    def pick(dst, c, w, src, hi, off, key, rd, rds, wr, wrs):
+        cp(T[dst][:, c:c + w].bitcast(dt.uint32), T[src][:, 0:hi].bitcast(dt.uint32).indirect(off), [key] + rd, wr)
+        act(T[dst + "_s"][:, c:c + w], T[src + "_s"][:, 0:hi].indirect(off), AF.Copy, [key] + rds, wrs)
+
+    def renew(t, side, k, b, c0):
+        o, key = 24 * t + 8 * k, "off%s%d" % (side, t)
+        off = T.offL[:, o:o + 8]
+        tt(T.lt[:, o:o + 8], bank(b, c0, c0 + 8), T.cl[:], OP.max, ["ps%d" % b, "cl"], ["lt%d" % o])
+        ts(off, T.lt[:, o:o + 8], float(BIG), None, ["lt%d" % o], [key], OP.add)
+        dst, c = ("win%s%d" % (side, t + 1), 0) if t < R - 1 else ("fin", 128 * "AHB".index(side))
+        pick(dst, c, P, "win%s%d" % (side, t), SLOT, off, key,
+             ["%s%d" % (side, t), "new%s%d" % (side, t)], ["%ss%d" % (side, t), "new%ss%d" % (side, t)],
+             ["%s%d" % (side, t + 1)], ["%ss%d" % (side, t + 1)])
+
+    def store(side, queues):
+        c = 128 * "AHB".index(side)
+        dma("y", T.oc[:, 4 * c:4 * c + 512], T.fin[:, c:c + 128].bitcast(dt.uint8), "sto", ["%s%d" % (side, R)], [])
+        for k in range(4):
+            dma(queues[k % len(queues)], T.osc[4 * k:4 * k + 4, c:c + 128], T.fin_s[32 * k:32 * k + 4, c:c + 128], "sto",
+                ["%ss%d" % (side, R)], [])
+
+    for b in range(4):
+        decode_own(0, b, True)
+    for t in range(R):
+        wh, qp = "winH%d" % t, "qp%d" % t
+        state_first(t)
+        state_second(t)
+        decode_own(t, 0, False)
+        decode_own(t, 1, False)
+        q_mx("dq", 0, 128, T.dr[:], ["dr0", "dr1", "dr2", "dr3"], ["dq"])
+        mm(0, "uq", 0, "dq", 0, True, True, ["uq", "dq"])
+        mm(1, "dq", 0, "uq", 0, True, True, ["uq", "dq"])
+        for b in range(4):
+            if b > 1:
+                decode_own(t, b, False)
+            mm(4 + b, "e1", 128 * b, "dq", 0, False, True, ["e1%d" % b, "dq"])
+        act(T.absS[:], bank(0), AF.Abs, ["ps0"], ["absS"])
+        op("v", lambda e: e.tensor_reduce(T.nac[:], bank(1, 0, 1), AxisListType.X, OP.max, negate=True,
+                                          apply_absolute_value=True), ["ps1"], ["nac"])
+        act(T.sgn[:], T.absS[:], AF.Sign, ["absS", "nac"], ["sgn"], bias=T.nac[:])
+        tt(T.bt[:], T.sgn[:], T.tri[:], OP.is_gt, ["sgn", "tri"], ["bt"])
+        op("v", lambda e: e.tensor_reduce(T.rk[:], T.bt[:], AxisListType.X, OP.add), ["bt"], ["rk"])
+        for b in range(3):
+            act(T.pt[:, b:512:4], bank(4 + b), AF.Copy, ["ps%d" % (4 + b)], ["pt%d" % b])
+        act(T.xt[:, 0:32:4], T.nmask8[:], AF.Relu, ["nmask8", "rk"], ["xt0"], bias=16.0, scale=T.rk[:])
+        act(T.xt[:, 1:32:4], T.mask8[:], AF.Relu, ["mask8", "rk"], ["xt1"], bias=-16.0, scale=T.rk[:])
+        act(T.xt[:, 2:32:4], T.mask8[:], AF.Relu, ["mask8", "rk"], ["xt2"], bias=-float(K - 1), scale=T.rk[:])
+        act(T.pt[:, 3:512:4], bank(7), AF.Copy, ["ps7"], ["pt3"])
+        ts(T.xt[:, 32:544], T.kk[:], T.rk[:], None, ["kk0", "kk1", "kk2", "kk3", "rk"], ["xtx"], OP.is_equal)
+        q_mx(wh, SLOT, WINH, T.xt[:], ["xt0", "xt1", "xt2", "xtx"], ["slotH%d" % t])
+        mm(2, wh, XC, "wcq", 2, True, True, ["wcq", "slotH%d" % t])
+        mm(3, "wcq", 0, wh, SLOT, True, True, ["wcq", "slotH%d" % t])
+        q_mx(qp, 0, 128, T.pt[:], ["pt0", "pt1", "pt2", "pt3"], [qp])
+        off = T.offE[:, 2 * t:2 * t + 2]
+        cp(off, bank(2, 126, 128), ["ps2"], ["offE%d" % t])
+        pick(wh, NEW, K, qp, P, off, "offE%d" % t, [qp], [qp], ["newH%d" % t], ["newHs%d" % t])
+
+        def send(kind, view):
+            tr = []
+            for dst, side in ((right, "A"), (left, "B")):
+                rid, pid = topo.addr(dst)[:2]
+                tr.append(RemoteDMATransfer(dst_ids=[DstId(rid=rid, pnc=pid)], dma_engine_mask=sum(1 << e for e in masks[dst]),
+                                            remote_sem=T.sem["%s%s%d" % (kind, side, t)],
+                                            src=view(wh), dst=view("win%s%d" % (side, t))))
+            g.remote_dma_fused(tr, local_sem=T.sem.sent)
+
+        depend("g", ["newH%d" % t, "slotH%d" % t], [])
+        send("c", lambda name: T[name][:, NEW:XC].bitcast(dt.uint8))
+        depend("g", ["newHs%d" % t, "slotH%d" % t], [])
+        send("s", lambda name: T[name + "_s"][:, NEW:XC])
+
+        renew(t, "H", 0, 3, 0)
+        cp(T.ech[:, 2 * t:2 * t + 2], bank(2, 126, 128), ["ps2"], ["ech%d" % t])
+        for q in range(2):
+            dma("y", T.ch[t:t + 1, 16 * q:16 * q + 16], T.ech[0:16, 2 * t + q:2 * t + q + 1], "sto", ["ech%d" % t], [])
+        if t < R - 1:
+            for b in range(4):
+                decode_own(t + 1, b, True)
+        else:
+            store("H", "y")
+            act(T.xef[:], T.xs[:], AF.Copy, ["xs0", "xs1", "xs2", "xs3"], ["xef"])
+            dma("y", T.xe[:], T.xef[:], "sto", ["xef"], [])
+        if t == 0:
+            q_mx("wq", 0, 128, T.wb[:], ["wb"], ["wq"])
+
+        for i, s in enumerate(order):
+            src = left if s == "A" else right
+            lands("new%s%d" % (s, t), "c%s%d" % (s, t), arrives(src))
+            lands("new%ss%d" % (s, t), "s%s%d" % (s, t), arrives(src))
+            mm(2 + i, "wcq", 0, "win%s%d" % (s, t), XC - 128, True, True,
+               ["wcq", "new%s%d" % (s, t), "new%ss%d" % (s, t)] + both(s, t))
+        for i, s in enumerate(order):
+            renew(t, s, 1 + i, 2 + i, 120)
+            if t == R - 1:
+                store(s, "sy")
+                if s == "A":
+                    mm(0, "wq", 0, "fin", 0, True, True, ["wq"] + both("A", R))
+                    cp(T.ysb[:], bank(0), ["ps0"], ["ysb"])
+                    dma("y", T.y[:], T.ysb[:], "sto", ["ysb"], [])
+
+    finish()
+    g.wait_ge(T.sem.sent, 2 * R * sum(len(m) for m in masks.values()))

@@ -2,25 +2,24 @@ from concourse.bass import DstId, RemoteDMATransfer
 from concourse.mybir import dt, AluOpType as OP, AxisListType, ActivationFunctionType as AF
 
 P, K, R = 128, 32, 3
-NEW, SLOT, XC = 128, 160, 168
-WIN, WINH = 168, 296
-CODE, BF, F32, U8 = "float8_e4m3fn_x4", "bfloat16", "float32", "uint8"
-BIG = 256
+NEW, SLOT, END = 128, 160, 168
+CODE, BF, F32, U8, I32 = "float8_e4m3fn_x4", "bfloat16", "float32", "uint8", "int32"
+BASE = P + K // 2
+FAR = 1024.0
 ZW = 520
 
 SCRATCH = {"ps": ("psum", [128, 4096], F32)}
 for _n, _w, _d in (("hlb", 512, BF), ("hcb", 512, BF), ("hrb", 512, BF), ("xs", 512, BF), ("wb", 512, BF), ("ub4", 4, BF),
-                   ("ubt", 512, BF), ("dr", 512, BF), ("pt", 512, BF), ("xt", 4 * 136, BF), ("ones", 128, BF),
-                   ("half", 128, BF), ("idm", 128, BF), ("tri", 128, BF), ("zd", 3 * ZW, BF), ("wc", 4 * 130, BF),
-                   ("kk", 512, BF), ("vj", 128, "int32"), ("vi", 128, "int32"), ("mask16", 128, BF), ("pq", 8, "int32"),
-                   ("pr", 8, "int32"), ("mask8", 8, F32), ("nmask8", 8, F32), ("pc", 1, "int32"), ("lo", 1, "int32"),
-                   ("hi", 1, "int32"), ("lof", 1, F32), ("cb", 8, F32), ("cl", 8, F32), ("absS", 128, F32),
-                   ("nac", 1, F32), ("sgn", 128, BF), ("bt", 128, BF), ("rk", 1, F32), ("offE", 2 * R, "uint16"),
-                   ("offL", 24 * R, "uint16"), ("lt", 24 * R, F32), ("ech", 2 * R, F32), ("xef", 512, F32),
-                   ("ysb", 128, F32)):
+                   ("ubt", 512, BF), ("dr", 512, BF), ("pt", 4 * 136, BF), ("xt", 512, BF), ("ones", 136, BF),
+                   ("idm", 128, BF), ("flip", 136, BF), ("zd", 3 * ZW, BF), ("wc", 4 * 130, BF), ("kk", 512, BF),
+                   ("row16", 128, BF), ("pc", 4, I32), ("lo", 2, I32), ("hi", 2, I32), ("p7", R, I32), ("hib", 1, BF),
+                   ("m1", 16, BF), ("m2", 16, BF), ("below", 8, BF), ("above", 16, BF), ("absS", 128, F32), ("ac", 1, F32),
+                   ("sgn", 128, BF), ("lg", 1, F32), ("eq", 136, BF), ("yy", 136, F32), ("offE", 4 * R, "uint16"),
+                   ("offL", 24 * R, "uint16"), ("ech", 2 * R, F32), ("xef", 512, F32), ("ysb", 160, F32), ("yp", 128, F32)):
     SCRATCH[_n] = ("sbuf", [128, _w], _d)
-for _n, _w in [("e1", 512), ("e25", 512), ("em5", 512), ("wcq", 130), ("uq", 128), ("wq", 128), ("dq", 128), ("fin", 384)] + [
-        ("%s%d" % (_a, _t), _b) for _t in range(R) for _a, _b in (("winA", WIN), ("winB", WIN), ("winH", WINH), ("qp", 128))]:
+for _n, _w in [("e1", 512), ("e25", 512), ("em5", 512), ("wcq", 130), ("uq", 128), ("wq", 128), ("dq", 128), ("xq", 128),
+               ("fin", 384)] + [("%s%d" % (_a, _t), _b) for _t in range(R)
+                                for _a, _b in (("winA", END), ("winB", END), ("winH", END + 8), ("qp", 136))]:
     SCRATCH[_n] = ("sbuf", [128, _w], CODE)
     SCRATCH[_n + "_s"] = ("sbuf", [128, _w], U8)
 
@@ -106,6 +105,7 @@ def rank_program(g, core, T, topo):
     n = len(cores)
     left, right = cores[(rank - 1) % n], cores[(rank + 1) % n]
     masks = _masks(topo, core, left, right)
+    sent = 2 * R * sum(len(m) for m in masks.values())
 
     def arrives(src):
         k = cores.index(src)
@@ -143,65 +143,67 @@ def rank_program(g, core, T, topo):
     def iota(out, pattern, base, cm, wr, **kw):
         op("g", lambda e: e.iota(out, pattern, base, cm, **kw), [], wr)
 
+    def choose(out, in_, pattern, cond, other, base, cm, rd, wr):
+        op("g", lambda e: e.affine_select(out, in_, pattern, cond, other, base, cm), rd, wr)
+
+    order = ["A", "B"]
+    if topo.chip(left) != topo.chip(core) and topo.chip(right) == topo.chip(core):
+        order = ["B", "A"]
+    first = {"A": "hl", "B": "hr"}
+
     dma("s", T.hcb[:], T.hc[:], "ldhc", [], ["hcb"])
-    dma("y", T.hlb[:], T.hl[:], "ldhl", [], ["hlb"])
-    dma("s", T.hrb[:], T.hr[:], "ldhr", [], ["hrb"])
+    dma("y", T[first[order[0]] + "b"][:], T[first[order[0]]][:], "ld" + first[order[0]], [], [first[order[0]] + "b"])
+    dma("s", T[first[order[1]] + "b"][:], T[first[order[1]]][:], "ld" + first[order[1]], [], [first[order[1]] + "b"])
+    dma("y", T.ub4[:], T.u[:, 0:4], "ldu", [], ["ub4"])
     dma("y", T.xs[:], T.x[:], "ldx", [], ["xs0", "xs1", "xs2", "xs3"])
-    dma("s", T.ub4[:], T.u[:, 0:4], "ldu", [], ["ub4"])
     dma("y", T.wb[:], T.w[:], "ldw", [], ["wb"])
 
     small = {"allow_small_or_imprecise_dtypes": True}
     fill(T.ones[:], 1.0, ["ones"])
     fill(T.zd[:, 0:ZW], 0.0, ["zd0"])
-    fill(T.half[:], -0.5, ["half"])
-    fill(T.wc[:, 3:512:4], 0.0, ["wcw3"])
     fill(T.wc[:, 512:520], 0.0, ["wcc"])
-    fill(T.xt[:, 0:32], 0.0, ["xt0", "xt1", "xt2"])
-    op("g", lambda e: e.affine_select(T.idm[:], T.ones[:], [[-1, 128]], OP.is_equal, 0.0, 0, 1), ["ones"], ["idm"])
-    iota(T.vj[:], [[-1, 128]], 128, 1, ["vj"])
-    iota(T.pc[:], [[0, 1]], 0, 1, ["pc"])
-    iota(T.pq[:], [[-16, 8]], 0, 1, ["pq"])
-    iota(T.cb[:], [[16, 8]], -BIG, 0, ["cb"], **small)
-    iota(T.kk[:, 0:64], [[1, 16], [0, 2], [16, 2]], 0, 0, ["kk0"], **small)
-    op("g", lambda e: e.affine_select(T.tri[:], T.half[:], [[-1, 128]], OP.is_gt, 0.5, 0, 1), ["half"], ["tri"])
+    iota(T.pc[:], [[0, 4]], 0, 1, ["pc"])
+    choose(T.idm[:], T.ones[:, 0:128], [[-1, 128]], OP.is_equal, 0.0, 0, 1, ["ones"], ["idm"])
+    iota(T.row16[:], [[0, 8], [1, 16]], 0, 0, ["row16"], **small)
+    iota(T.kk[:, 0:64], [[2, 16], [0, 2], [K, 2]], -K, 0, ["kk0"], **small)
+    choose(T.m1[:], T.ones[:, 0:16], [[-16, 8], [0, 2]], OP.is_ge, 0.0, 0, 1, ["ones"], ["m1"])
+    choose(T.m2[:], T.m1[:], [[16, 8], [0, 2]], OP.is_ge, 0.0, 15, -1, ["m1"], ["m2"])
+    choose(T.flip[:], T.ones[:], [[-1, 136]], OP.not_equal, -1.0, 1, 1, ["ones"], ["flip"])
     act(T.zd[:, 3:515:4], T.idm[:], AF.Copy, ["idm"], ["zd0"])
     for f, s in ((1, 0.25), (2, -0.5)):
         act(T.zd[:, ZW * f:ZW * f + ZW], T.zd[:, 0:ZW], AF.Copy, ["zd0"], ["zd%d" % f], scale=s)
+    for k, w in ((1, 64), (2, 128), (3, 256)):
+        act(T.kk[:, w:2 * w], T.kk[:, 0:w], AF.Copy, ["kk%d" % j for j in range(k)], ["kk%d" % k])
+    act(T.below[:], T.m2[:, 0:16:2], AF.Identity, ["m2"], ["below"], scale=FAR + K, bias=-FAR)
+    act(T.above[:], T.m2[:], AF.Identity, ["m2"], ["above"], scale=K - FAR, bias=FAR)
+    for t in range(4):
+        act(T.ubt[:, t:512:4], T.ones[:, 0:128], AF.Identity, ["ones", "ub4"], ["ubt%d" % t], scale=0.0, bias=T.ub4[:, t:t + 1])
 
     def decoders(f, name):
         for b in range(4):
             q_mx(name, 128 * b, 128 * b + 128, T.zd[:, ZW * f + 3 - b:ZW * f + 515 - b], ["zd%d" % f], ["%s%d" % (name, b)])
 
+    ts(T.lo[:], T.pc[:, 0:2], 15, None, ["pc"], ["lo"], OP.bitwise_and)
+    ts(T.hi[:], T.pc[:, 0:2], 112, None, ["pc"], ["hi"], OP.bitwise_and)
+    ts(T.p7[:], T.pc[:, 0:R], 7, None, ["pc"], ["p7"], OP.bitwise_and)
+    cp(T.wc[:, 512:518:5], T.lo[:], ["lo"], ["wcc"])
+    cp(T.wc[:, 514:520:5], T.hi[:], ["hi"], ["wcc"])
+    ts(T.offE[:, 2:4 * R:4], T.p7[:], float(P), None, ["p7"], ["offS"], OP.add)
+    ts(T.hib[:], T.hi[:, 0:1], -float(BASE), None, ["hi"], ["hib"], OP.add)
     decoders(0, "e1")
-    ts(T.vi[:], T.vj[:], 15, None, ["vj"], ["vi"], OP.bitwise_and)
-    ts(T.pr[:], T.pq[:], 4, None, ["pq"], ["pr"], OP.arith_shift_right)
-    ts(T.lo[:], T.pc[:], 15, None, ["pc"], ["lo"], OP.bitwise_and)
-    ts(T.hi[:], T.pc[:], 112, None, ["pc"], ["hi"], OP.bitwise_and)
-    ts(T.mask16[:], T.vi[:], 0, None, ["vi"], ["mask16"], OP.is_equal)
-    ts(T.mask8[:], T.pr[:], 0, None, ["pr"], ["mask8"], OP.is_equal)
-    cp(T.lof[:], T.lo[:], ["lo"], ["lof"])
-    for c, name in ((0, "lo"), (2, "hi"), (5, "lo"), (7, "hi")):
-        cp(T.wc[:, 512 + c:513 + c], T[name][:], [name], ["wcc"])
-    ts(T.cl[:], T.cb[:], T.lof[:], None, ["cb", "lof"], ["cl"], OP.add)
-    for t, s in ((0, -1.0), (1, 1.0), (2, -float(BIG))):
-        act(T.wc[:, t:512:4], T.mask16[:], AF.Copy, ["mask16"], ["wcw%d" % t], scale=s)
-    act(T.nmask8[:], T.mask8[:], AF.Copy, ["mask8"], ["nmask8"], scale=-1.0)
-    for k, w in ((1, 64), (2, 128), (3, 256)):
-        act(T.kk[:, w:2 * w], T.kk[:, 0:w], AF.Copy, ["kk%d" % j for j in range(k)], ["kk%d" % k])
     decoders(1, "e25")
-    decoders(2, "em5")
-    q_mx("wcq", 0, 130, T.wc[:], ["wcw0", "wcw1", "wcw2", "wcw3", "wcc"], ["wcq"])
+    low = T.wc[:, 512:513]
+    for t, s in ((0, 0.5), (1, T.hib[:]), (2, 0.0), (3, low)):
+        ts(T.wc[:, t:512:4], T.row16[:], low, s, ["row16", "wcc", "hib"], ["wcw%d" % t], OP.is_equal, OP.mult)
+    fill(T.pt[:, 512:544], 0.0, ["sl0", "sl1"])
+    fill(T.eq[:, 0:1], -float(P - K), ["eq0"])
 
     q_mx("winH0", 0, 128, T.hcb[:], ["hcb"], ["H0", "Hs0"])
-    q_mx("winA0", 0, 128, T.hlb[:], ["hlb"], ["A0", "As0"])
-    q_mx("winB0", 0, 128, T.hrb[:], ["hrb"], ["B0", "Bs0"])
-    for t in range(4):
-        ts(T.ubt[:, t:512:4], T.ones[:], T.ub4[:, t:t + 1], None, ["ones", "ub4"], ["ubt%d" % t], OP.mult)
+    decoders(2, "em5")
+    for s in order:
+        q_mx("win%s0" % s, 0, 128, T[first[s] + "b"][:], [first[s] + "b"], ["%s0" % s, "%ss0" % s])
+    q_mx("wcq", 0, 130, T.wc[:], ["wcw0", "wcw1", "wcw2", "wcw3", "wcc"], ["wcq"])
     q_mx("uq", 0, 128, T.ubt[:], ["ubt0", "ubt1", "ubt2", "ubt3"], ["uq"])
-
-    order = ["A", "B"]
-    if topo.chip(left) != topo.chip(core) and topo.chip(right) == topo.chip(core):
-        order = ["B", "A"]
 
     def both(side, t):
         return ["%s%d" % (side, t), "%ss%d" % (side, t)]
@@ -214,24 +216,29 @@ def rank_program(g, core, T, topo):
         for b in range(4):
             mm(b, "e25", 128 * b, "win%s%d" % (order[1], t), 0, False, False, ["e25%d" % b] + both(order[1], t))
             mm(b, "em5", 128 * b, "winH%d" % t, 0, False, True, ["em5%d" % b] + both("H", t))
-            xb, db = T.xs[:, b:512:4], T.dr[:, b:512:4]
+            xb = T.xs[:, b:512:4]
             tt(xb, xb, bank(b), OP.add, ["xs%d" % b, "ps%d" % b], ["xs%d" % b])
-            tt(db, xb, bank(4 + b), OP.subtract, ["xs%d" % b, "ps%d" % (4 + b)], ["dr%d" % b])
+            if t == R - 1:
+                act(T.xef[:, b:512:4], xb, AF.Copy, ["xs%d" % b], ["xef%d" % b])
+            for k in ([b - 1] if b else []) + ([b] if b == 3 else []):
+                tt(T.dr[:, k:512:4], T.xs[:, k:512:4], bank(4 + k), OP.subtract, ["xs%d" % k, "ps%d" % (4 + k)], ["dr%d" % k])
 
     def decode_own(t, b, alone):
         mm(4 + b, "e1", 128 * b, "winH%d" % t, 0, True, alone, ["e1%d" % b] + both("H", t))
 
-    def pick(dst, c, w, src, hi, off, key, rd, rds, wr, wrs):
-        cp(T[dst][:, c:c + w].bitcast(dt.uint32), T[src][:, 0:hi].bitcast(dt.uint32).indirect(off), [key] + rd, wr)
-        act(T[dst + "_s"][:, c:c + w], T[src + "_s"][:, 0:hi].indirect(off), AF.Copy, [key] + rds, wrs)
+    def pick(dst, c, w, src, hi, off, keys, rd, rds, wr, wrs):
+        cp(T[dst][:, c:c + w].bitcast(dt.uint32), T[src][:, 0:hi].bitcast(dt.uint32).indirect(off), keys + rd, wr)
+        act(T[dst + "_s"][:, c:c + w], T[src + "_s"][:, 0:hi].indirect(off), AF.Copy, keys + rds, wrs)
 
-    def renew(t, side, k, b, c0):
-        o, key = 24 * t + 8 * k, "off%s%d" % (side, t)
-        off = T.offL[:, o:o + 8]
-        tt(T.lt[:, o:o + 8], bank(b, c0, c0 + 8), T.cl[:], OP.max, ["ps%d" % b, "cl"], ["lt%d" % o])
-        ts(off, T.lt[:, o:o + 8], float(BIG), None, ["lt%d" % o], [key], OP.add)
+    def list_of(t, side, lo=0, hi=8):
+        k = 24 * t + 8 * "HAB".index(side)
+        return T.offL[:, k + lo:k + hi], "off%s%d" % (side, t)
+
+    def renew(t, side, b):
+        off, key = list_of(t, side)
+        ts(off, bank(b, 120, 128), float(BASE), None, ["ps%d" % b], [key], OP.add)
         dst, c = ("win%s%d" % (side, t + 1), 0) if t < R - 1 else ("fin", 128 * "AHB".index(side))
-        pick(dst, c, P, "win%s%d" % (side, t), SLOT, off, key,
+        pick(dst, c, P, "win%s%d" % (side, t), SLOT, off, [key],
              ["%s%d" % (side, t), "new%s%d" % (side, t)], ["%ss%d" % (side, t), "new%ss%d" % (side, t)],
              ["%s%d" % (side, t + 1)], ["%ss%d" % (side, t + 1)])
 
@@ -248,35 +255,35 @@ def rank_program(g, core, T, topo):
         wh, qp = "winH%d" % t, "qp%d" % t
         state_first(t)
         state_second(t)
-        decode_own(t, 0, False)
-        decode_own(t, 1, False)
+        for b in range(3):
+            decode_own(t, b, False)
         q_mx("dq", 0, 128, T.dr[:], ["dr0", "dr1", "dr2", "dr3"], ["dq"])
         mm(0, "uq", 0, "dq", 0, True, True, ["uq", "dq"])
         mm(1, "dq", 0, "uq", 0, True, True, ["uq", "dq"])
         for b in range(4):
-            if b > 1:
+            if b == 3:
                 decode_own(t, b, False)
             mm(4 + b, "e1", 128 * b, "dq", 0, False, True, ["e1%d" % b, "dq"])
+        op("v", lambda e: e.tensor_reduce(T.ac[:], bank(1, 0, 1), AxisListType.X, OP.max, apply_absolute_value=True),
+           ["ps1"], ["ac"])
         act(T.absS[:], bank(0), AF.Abs, ["ps0"], ["absS"])
-        op("v", lambda e: e.tensor_reduce(T.nac[:], bank(1, 0, 1), AxisListType.X, OP.max, negate=True,
-                                          apply_absolute_value=True), ["ps1"], ["nac"])
-        act(T.sgn[:], T.absS[:], AF.Sign, ["absS", "nac"], ["sgn"], bias=T.nac[:])
-        tt(T.bt[:], T.sgn[:], T.tri[:], OP.is_gt, ["sgn", "tri"], ["bt"])
-        op("v", lambda e: e.tensor_reduce(T.rk[:], T.bt[:], AxisListType.X, OP.add), ["bt"], ["rk"])
-        for b in range(3):
+        act(T.sgn[:], T.absS[:], AF.Sign, ["absS", "ac"], ["sgn", "lg"], scale=-1.0, bias=T.ac[:], accum_out=T.lg[:])
+        ts(T.eq[:, 1:129], T.absS[:], T.ac[:], -1.0, ["absS", "ac"], ["eq"], OP.is_equal, OP.mult)
+        op("v", lambda e: e.tensor_tensor_scan(T.yy[:, 0:129], T.flip[:, 0:129], T.eq[:, 0:129], T.lg[:], OP.mult, OP.add),
+           ["flip", "eq0", "eq", "lg"], ["yy"])
+        y = T.yy[:, 128:129]
+        for b in range(4):
             act(T.pt[:, b:512:4], bank(4 + b), AF.Copy, ["ps%d" % (4 + b)], ["pt%d" % b])
-        act(T.xt[:, 0:32:4], T.nmask8[:], AF.Relu, ["nmask8", "rk"], ["xt0"], bias=16.0, scale=T.rk[:])
-        act(T.xt[:, 1:32:4], T.mask8[:], AF.Relu, ["mask8", "rk"], ["xt1"], bias=-16.0, scale=T.rk[:])
-        act(T.xt[:, 2:32:4], T.mask8[:], AF.Relu, ["mask8", "rk"], ["xt2"], bias=-float(K - 1), scale=T.rk[:])
-        act(T.pt[:, 3:512:4], bank(7), AF.Copy, ["ps7"], ["pt3"])
-        ts(T.xt[:, 32:544], T.kk[:], T.rk[:], None, ["kk0", "kk1", "kk2", "kk3", "rk"], ["xtx"], OP.is_equal)
-        q_mx(wh, SLOT, WINH, T.xt[:], ["xt0", "xt1", "xt2", "xtx"], ["slotH%d" % t])
-        mm(2, wh, XC, "wcq", 2, True, True, ["wcq", "slotH%d" % t])
-        mm(3, "wcq", 0, wh, SLOT, True, True, ["wcq", "slotH%d" % t])
-        q_mx(qp, 0, 128, T.pt[:], ["pt0", "pt1", "pt2", "pt3"], [qp])
-        off = T.offE[:, 2 * t:2 * t + 2]
-        cp(off, bank(2, 126, 128), ["ps2"], ["offE%d" % t])
-        pick(wh, NEW, K, qp, P, off, "offE%d" % t, [qp], [qp], ["newH%d" % t], ["newHs%d" % t])
+        ts(T.xt[:], T.kk[:], y, None, ["kk0", "kk1", "kk2", "kk3", "yy"], ["xt"], OP.is_equal)
+        ts(T.pt[:, 512:544:4], T.below[:], y, y, ["below", "yy"], ["sl0"], OP.is_gt, OP.mult)
+        q_mx("xq", 0, 128, T.xt[:], ["xt"], ["xq"])
+        mm(2, "xq", 0, "wcq", 2, True, True, ["wcq", "xq"])
+        ts(T.pt[:, 513:544:2], T.above[:], y, None, ["above", "yy"], ["sl1"], OP.is_le)
+        q_mx(qp, 0, 136, T.pt[:], ["pt0", "pt1", "pt2", "pt3", "sl0", "sl1"], [qp])
+        mm(3, "wcq", 0, qp, 8, True, True, ["wcq", qp])
+        cp(T.offE[:, 4 * t:4 * t + 2], bank(2, 126, 128), ["ps2"], ["offE%d" % t])
+        pick(wh, NEW, K + 16, qp, 136, T.offE[:, 4 * t:4 * t + 3], ["offE%d" % t, "offS"], [qp], [qp],
+             ["newH%d" % t], ["newHs%d" % t])
 
         def send(kind, view):
             tr = []
@@ -287,13 +294,17 @@ def rank_program(g, core, T, topo):
                                             src=view(wh), dst=view("win%s%d" % (side, t))))
             g.remote_dma_fused(tr, local_sem=T.sem.sent)
 
-        depend("g", ["newH%d" % t, "slotH%d" % t], [])
-        send("c", lambda name: T[name][:, NEW:XC].bitcast(dt.uint8))
-        depend("g", ["newHs%d" % t, "slotH%d" % t], [])
-        send("s", lambda name: T[name + "_s"][:, NEW:XC])
+        depend("g", ["newH%d" % t], [])
+        send("c", lambda name: T[name][:, NEW:END].bitcast(dt.uint8))
+        depend("g", ["newHs%d" % t], [])
+        send("s", lambda name: T[name + "_s"][:, NEW:END])
 
-        renew(t, "H", 0, 3, 0)
+        renew(t, "H", 3)
         cp(T.ech[:, 2 * t:2 * t + 2], bank(2, 126, 128), ["ps2"], ["ech%d" % t])
+        if t == 0:
+            q_mx("wq", 0, 128, T.wb[:], ["wb"], ["wq"])
+        if t == R - 1:
+            g.sync.wait_ge(T.sem.sent, sent)
         for q in range(2):
             dma("y", T.ch[t:t + 1, 16 * q:16 * q + 16], T.ech[0:16, 2 * t + q:2 * t + q + 1], "sto", ["ech%d" % t], [])
         if t < R - 1:
@@ -301,25 +312,30 @@ def rank_program(g, core, T, topo):
                 decode_own(t + 1, b, True)
         else:
             store("H", "y")
-            act(T.xef[:], T.xs[:], AF.Copy, ["xs0", "xs1", "xs2", "xs3"], ["xef"])
-            dma("y", T.xe[:], T.xef[:], "sto", ["xef"], [])
-        if t == 0:
-            q_mx("wq", 0, 128, T.wb[:], ["wb"], ["wq"])
+            dma("y", T.xe[:], T.xef[:], "sto", ["xef%d" % b for b in range(4)], [])
+            mm(0, "wq", 0, "winA%d" % t, 0, True, True, ["wq"] + both("A", t))
+            act(T.ysb[:, 0:P], bank(0), AF.Copy, ["ps0"], ["ysb0"])
 
         for i, s in enumerate(order):
             src = left if s == "A" else right
             lands("new%s%d" % (s, t), "c%s%d" % (s, t), arrives(src))
             lands("new%ss%d" % (s, t), "s%s%d" % (s, t), arrives(src))
-            mm(2 + i, "wcq", 0, "win%s%d" % (s, t), XC - 128, True, True,
-               ["wcq", "new%s%d" % (s, t), "new%ss%d" % (s, t)] + both(s, t))
+            new = ["new%s%d" % (s, t), "new%ss%d" % (s, t)] + both(s, t)
+            mm(2 + i, "wcq", 0, "win%s%d" % (s, t), END - 128, True, True, ["wcq"] + new)
+            if t == R - 1 and s == "A":
+                mm(1, "wq", 0, "winA%d" % t, END - 128, True, True, ["wq"] + new)
         for i, s in enumerate(order):
-            renew(t, s, 1 + i, 2 + i, 120)
+            if t == R - 1 and s == "A":
+                act(T.ysb[:, P:P + K], bank(1, 88, 120), AF.Copy, ["ps1"], ["ysb1"])
+            renew(t, s, 2 + i)
+            if t == R - 1 and s == "A":
+                (off0, key), (off1, key) = list_of(t, s, 0, 4), list_of(t, s, 4, 8)
+                cp(T.yp[:, 0:64], T.ysb[:].indirect(off0), ["ysb0", "ysb1", key], ["yp0"])
+                act(T.yp[:, 64:P], T.ysb[:].indirect(off1), AF.Copy, ["ysb0", "ysb1", key], ["yp1"])
             if t == R - 1:
                 store(s, "sy")
                 if s == "A":
-                    mm(0, "wq", 0, "fin", 0, True, True, ["wq"] + both("A", R))
-                    cp(T.ysb[:], bank(0), ["ps0"], ["ysb"])
-                    dma("y", T.y[:], T.ysb[:], "sto", ["ysb"], [])
+                    dma("y", T.y[:], T.yp[:], "sto", ["yp0", "yp1"], [])
 
     finish()
-    g.wait_ge(T.sem.sent, 2 * R * sum(len(m) for m in masks.values()))
+    g.wait_ge(T.sem.sent, sent)

@@ -2,29 +2,31 @@ from concourse.bass import DstId, RemoteDMATransfer
 from concourse.mybir import dt, AluOpType as OP, AxisListType, ActivationFunctionType as AF
 
 P, K, R = 128, 32, 3
-NEW, SLOT, END = 128, 160, 168
+NEW, END = P, P + K
+ROOM = 16
+NS = ROOM // 4
+XW = P + ROOM
 CODE, BF, F32, U8, I32 = "float8_e4m3fn_x4", "bfloat16", "float32", "uint8", "int32"
-BASE = P + K // 2
 FAR = 1024.0
 ZW = 520
 
 SCRATCH = {"ps": ("psum", [128, 4096], F32)}
 for _n, _w, _d in (("hlb", 512, BF), ("hcb", 512, BF), ("hrb", 512, BF), ("xs", 512, BF), ("wb", 512, BF), ("ub4", 4, BF),
-                   ("ubt", 512, BF), ("dr", 512, BF), ("pt", 4 * 136, BF), ("xt", 512, BF), ("ones", 136, BF),
-                   ("idm", 128, BF), ("flip", 136, BF), ("zd", 3 * ZW, BF), ("wc", 4 * 130, BF), ("kk", 512, BF),
-                   ("row16", 128, BF), ("pc", 4, I32), ("lo", 2, I32), ("hi", 2, I32), ("p7", R, I32), ("hib", 1, BF),
-                   ("m1", 16, BF), ("m2", 16, BF), ("below", 8, BF), ("above", 16, BF), ("absS", 128, F32), ("ac", 1, F32),
-                   ("sgn", 128, BF), ("lg", 1, F32), ("eq", 136, BF), ("yy", 136, F32), ("offE", 4 * R, "uint16"),
-                   ("offL", 24 * R, "uint16"), ("ech", 2 * R, F32), ("xef", 512, F32), ("ysb", 160, F32), ("yp", 128, F32)):
+                   ("ubt", 512, BF), ("dr", 512, BF), ("pt", 512, BF), ("xt", 4 * XW, BF), ("ones", 136, BF),
+                   ("idm", 128, BF), ("flip", 136, BF), ("zd", 3 * ZW, BF), ("wc", 4 * 134, BF), ("kk", 256, BF),
+                   ("row16", 128, BF), ("pc", 4, I32), ("lo", 2, I32), ("hi", 2, I32), ("c16", 8, F32), ("pnum", 8, F32),
+                   ("m1", 8, BF), ("m2", 8, BF), ("below", 8, BF), ("absS", 128, F32), ("ac", 1, F32),
+                   ("sgn", 128, BF), ("lg", 1, F32), ("eq", 136, BF), ("yy", 136, BF), ("offE", 2 * R, "uint16"),
+                   ("lst", 24, F32), ("offL", 24 * R, "uint16"), ("ech", 2 * R, F32), ("xef", 512, F32), ("yp", 128, F32)):
     SCRATCH[_n] = ("sbuf", [128, _w], _d)
-for _n, _w in [("e1", 512), ("e25", 512), ("em5", 512), ("wcq", 130), ("uq", 128), ("wq", 128), ("dq", 128), ("xq", 128),
-               ("fin", 384)] + [("%s%d" % (_a, _t), _b) for _t in range(R)
-                                for _a, _b in (("winA", END), ("winB", END), ("winH", END + 8), ("qp", 136))]:
+for _n, _w in [("e1", 512), ("e25", 512), ("em5", 512), ("wcq", 134), ("ws1", 128), ("uq", 128), ("wq", 128), ("dq", 128),
+               ("fin", 384)] + [("%s%d" % (_a, _t), _b) for _t in range(R) for _a, _b in (
+                   ("winA", END), ("winB", END), ("winH", END), ("qp", 128), ("xq", XW), ("slA", XW), ("slB", XW))]:
     SCRATCH[_n] = ("sbuf", [128, _w], CODE)
     SCRATCH[_n + "_s"] = ("sbuf", [128, _w], U8)
 
 SEMAPHORES = ["sv", "ss", "sp", "sg", "sent", "sto"] + ["ld" + n for n in ("hl", "hc", "hr", "x", "w", "u")] + [
-    "%s%s%d" % (k, s, t) for k in "cs" for s in "AB" for t in range(R)]
+    "%s%s%d" % (k, s, t) for k in "ocs" for s in "AB" for t in range(R)]
 
 
 def _flow(g, T):
@@ -105,7 +107,7 @@ def rank_program(g, core, T, topo):
     n = len(cores)
     left, right = cores[(rank - 1) % n], cores[(rank + 1) % n]
     masks = _masks(topo, core, left, right)
-    sent = 2 * R * sum(len(m) for m in masks.values())
+    sent = 3 * R * sum(len(m) for m in masks.values())
 
     def arrives(src):
         k = cores.index(src)
@@ -120,9 +122,9 @@ def rank_program(g, core, T, topo):
     def q_mx(name, a, b, tile, rd, wr):
         op("v", lambda e: e.quantize_mx(T[name][:, a:b], T[name + "_s"][:, a:b], tile), rd, wr)
 
-    def mm(b, ln, la, rn, ra, start, stop, rd):
-        op("p", lambda e: e.matmul_mx(bank(b), T[ln][:, la:la + 128], T[ln + "_s"][:, la:la + 128],
-                                      T[rn][:, ra:ra + 128], T[rn + "_s"][:, ra:ra + 128], start, stop),
+    def mm(b, ln, la, rn, ra, start, stop, rd, w=128):
+        op("p", lambda e: e.matmul_mx(bank(b, 0, w), T[ln][:, la:la + 128], T[ln + "_s"][:, la:la + 128],
+                                      T[rn][:, ra:ra + w], T[rn + "_s"][:, ra:ra + w], start, stop),
            rd, ["ps%d" % b])
 
     def act(out, in_, func, rd, wr, **kw):
@@ -160,50 +162,54 @@ def rank_program(g, core, T, topo):
 
     small = {"allow_small_or_imprecise_dtypes": True}
     fill(T.ones[:], 1.0, ["ones"])
-    fill(T.zd[:, 0:ZW], 0.0, ["zd0"])
-    fill(T.wc[:, 512:520], 0.0, ["wcc"])
-    iota(T.pc[:], [[0, 4]], 0, 1, ["pc"])
+    for f in range(3):
+        fill(T.zd[:, ZW * f:ZW * f + ZW], 0.0, ["zd%d" % f])
     choose(T.idm[:], T.ones[:, 0:128], [[-1, 128]], OP.is_equal, 0.0, 0, 1, ["ones"], ["idm"])
+    iota(T.pc[:], [[0, 4]], 0, 1, ["pc"])
     iota(T.row16[:], [[0, 8], [1, 16]], 0, 0, ["row16"], **small)
-    iota(T.kk[:, 0:64], [[2, 16], [0, 2], [K, 2]], -K, 0, ["kk0"], **small)
-    choose(T.m1[:], T.ones[:, 0:16], [[-16, 8], [0, 2]], OP.is_ge, 0.0, 0, 1, ["ones"], ["m1"])
-    choose(T.m2[:], T.m1[:], [[16, 8], [0, 2]], OP.is_ge, 0.0, 15, -1, ["m1"], ["m2"])
+    for c in range(2):
+        iota(T.kk[:, 128 * c:128 * c + 128], [[0, 8], [2, 16]], K * (c - 1), 0, ["kk%d" % c], **small)
+    choose(T.m1[:], T.ones[:, 0:8], [[-16, NS], [-16 * NS, 2]], OP.is_ge, 0.0, 0, 1, ["ones"], ["m1"])
+    choose(T.m2[:], T.m1[:], [[16, NS], [16 * NS, 2]], OP.is_ge, 0.0, 15, -1, ["m1"], ["m2"])
     choose(T.flip[:], T.ones[:], [[-1, 136]], OP.not_equal, -1.0, 1, 1, ["ones"], ["flip"])
-    act(T.zd[:, 3:515:4], T.idm[:], AF.Copy, ["idm"], ["zd0"])
+    iota(T.c16[:], [[16, 8]], 0, 0, ["c16"], **small)
+    cp(T.zd[:, 3:515:4], T.idm[:], ["idm"], ["zd0"])
     for f, s in ((1, 0.25), (2, -0.5)):
-        act(T.zd[:, ZW * f:ZW * f + ZW], T.zd[:, 0:ZW], AF.Copy, ["zd0"], ["zd%d" % f], scale=s)
-    for k, w in ((1, 64), (2, 128), (3, 256)):
-        act(T.kk[:, w:2 * w], T.kk[:, 0:w], AF.Copy, ["kk%d" % j for j in range(k)], ["kk%d" % k])
-    act(T.below[:], T.m2[:, 0:16:2], AF.Identity, ["m2"], ["below"], scale=FAR + K, bias=-FAR)
-    act(T.above[:], T.m2[:], AF.Identity, ["m2"], ["above"], scale=K - FAR, bias=FAR)
+        act(T.zd[:, ZW * f + 3:ZW * f + 515:4], T.idm[:], AF.Copy, ["idm"], ["zd%d" % f], scale=s)
     for t in range(4):
         act(T.ubt[:, t:512:4], T.ones[:, 0:128], AF.Identity, ["ones", "ub4"], ["ubt%d" % t], scale=0.0, bias=T.ub4[:, t:t + 1])
+    act(T.below[:], T.m2[:], AF.Identity, ["m2"], ["below"], scale=FAR + K, bias=-FAR)
+
+    low = T.wc[:, 520:521]
 
     def decoders(f, name):
         for b in range(4):
             q_mx(name, 128 * b, 128 * b + 128, T.zd[:, ZW * f + 3 - b:ZW * f + 515 - b], ["zd%d" % f], ["%s%d" % (name, b)])
 
-    ts(T.lo[:], T.pc[:, 0:2], 15, None, ["pc"], ["lo"], OP.bitwise_and)
-    ts(T.hi[:], T.pc[:, 0:2], 112, None, ["pc"], ["hi"], OP.bitwise_and)
-    ts(T.p7[:], T.pc[:, 0:R], 7, None, ["pc"], ["p7"], OP.bitwise_and)
-    cp(T.wc[:, 512:518:5], T.lo[:], ["lo"], ["wcc"])
-    cp(T.wc[:, 514:520:5], T.hi[:], ["hi"], ["wcc"])
-    ts(T.offE[:, 2:4 * R:4], T.p7[:], float(P), None, ["p7"], ["offS"], OP.add)
-    ts(T.hib[:], T.hi[:, 0:1], -float(BASE), None, ["hi"], ["hib"], OP.add)
     decoders(0, "e1")
-    decoders(1, "e25")
-    low = T.wc[:, 512:513]
-    for t, s in ((0, 0.5), (1, T.hib[:]), (2, 0.0), (3, low)):
-        ts(T.wc[:, t:512:4], T.row16[:], low, s, ["row16", "wcc", "hib"], ["wcw%d" % t], OP.is_equal, OP.mult)
-    fill(T.pt[:, 512:544], 0.0, ["sl0", "sl1"])
-    fill(T.eq[:, 0:1], -float(P - K), ["eq0"])
-
     q_mx("winH0", 0, 128, T.hcb[:], ["hcb"], ["H0", "Hs0"])
-    decoders(2, "em5")
+    decoders(1, "e25")
     for s in order:
         q_mx("win%s0" % s, 0, 128, T[first[s] + "b"][:], [first[s] + "b"], ["%s0" % s, "%ss0" % s])
-    q_mx("wcq", 0, 130, T.wc[:], ["wcw0", "wcw1", "wcw2", "wcw3", "wcc"], ["wcq"])
+        if s == order[0]:
+            fill(T.wc[:], 0.0, ["wcc", "wcw0", "wcw1"])
+            fill(T.xt[:], 0.0, ["xt0", "xt1", "xt2", "wrA", "wrB"])
+            fill(T.eq[:, 0:1], -float(P - K), ["eq0"])
+            ts(T.lo[:], T.pc[:, 0:2], 15, None, ["pc"], ["lo"], OP.bitwise_and)
+            ts(T.hi[:], T.pc[:, 0:2], 112, None, ["pc"], ["hi"], OP.bitwise_and)
+            cp(T.wc[:, 520:526:5], T.lo[:], ["lo"], ["wcc"])
+            cp(T.wc[:, 528:534:5], T.hi[:], ["hi"], ["wcc"])
+    decoders(2, "em5")
     q_mx("uq", 0, 128, T.ubt[:], ["ubt0", "ubt1", "ubt2", "ubt3"], ["uq"])
+
+    def late_constants():
+        ts(T.wc[:, 2:512:4], T.row16[:], low, 0.5, ["row16", "wcc"], ["wcw0"], OP.is_equal, OP.mult)
+        ts(T.wc[:, 3:512:4], T.row16[:], low, None, ["row16", "wcc"], ["wcw1"], OP.is_equal)
+        act(T.pnum[:], T.c16[:], AF.Identity, ["c16", "wcc"], ["pnum"], bias=low)
+
+    def late_tiles():
+        q_mx("wcq", 0, 134, T.wc[:], ["wcw0", "wcw1", "wcc"], ["wcq"])
+        q_mx("ws1", 0, 128, T.wc[:, 2:514], ["wcw0", "wcw1", "wcc"], ["ws1"])
 
     def both(side, t):
         return ["%s%d" % (side, t), "%ss%d" % (side, t)]
@@ -230,36 +236,57 @@ def rank_program(g, core, T, topo):
         cp(T[dst][:, c:c + w].bitcast(dt.uint32), T[src][:, 0:hi].bitcast(dt.uint32).indirect(off), keys + rd, wr)
         act(T[dst + "_s"][:, c:c + w], T[src + "_s"][:, 0:hi].indirect(off), AF.Copy, keys + rds, wrs)
 
-    def list_of(t, side, lo=0, hi=8):
+    def list_of(t, side):
         k = 24 * t + 8 * "HAB".index(side)
-        return T.offL[:, k + lo:k + hi], "off%s%d" % (side, t)
+        return T.offL[:, k:k + 8], "off%s%d" % (side, t)
 
-    def renew(t, side, b):
+    def beside(t, side):
+        name = "sl%s%d" % (side, t)
+        q_mx(name, 0, P, T.dr[:], ["dr0", "dr1", "dr2", "dr3"], ["by" + name])
+
+    def sums(t, side, b):
+        name = "xq%d" % t if side == "H" else "sl%s%d" % (side, t)
+        rd = [name] if side == "H" else [name, "by" + name]
+        mm(b, "wcq", 0, name, 0, True, True, ["wcq"] + rd, P + NS)
+        mm(b, "ws1", 0, name, NS, True, True, ["ws1"] + rd)
+
+    def make_list(t, side, b):
         off, key = list_of(t, side)
-        ts(off, bank(b, 120, 128), float(BASE), None, ["ps%d" % b], [key], OP.add)
+        k = 8 * "HAB".index(side)
+        f = T.lst[:, k:k + 8]
+        tt(f, bank(b, P - NS, P + NS), T.pnum[:], OP.max, ["ps%d" % b, "pnum"], ["lst" + side])
+        cp(off, f, ["lst" + side], [key])
+
+    def renew(t, side):
+        off, key = list_of(t, side)
         dst, c = ("win%s%d" % (side, t + 1), 0) if t < R - 1 else ("fin", 128 * "AHB".index(side))
-        pick(dst, c, P, "win%s%d" % (side, t), SLOT, off, [key],
+        pick(dst, c, P, "win%s%d" % (side, t), END, off, [key],
              ["%s%d" % (side, t), "new%s%d" % (side, t)], ["%ss%d" % (side, t), "new%ss%d" % (side, t)],
              ["%s%d" % (side, t + 1)], ["%ss%d" % (side, t + 1)])
 
-    def store(side, queues):
+    def store_codes(side):
         c = 128 * "AHB".index(side)
         dma("y", T.oc[:, 4 * c:4 * c + 512], T.fin[:, c:c + 128].bitcast(dt.uint8), "sto", ["%s%d" % (side, R)], [])
-        for k in range(4):
-            dma(queues[k % len(queues)], T.osc[4 * k:4 * k + 4, c:c + 128], T.fin_s[32 * k:32 * k + 4, c:c + 128], "sto",
-                ["%ss%d" % (side, R)], [])
+
+    def store_scales(side, q, ks):
+        c = 128 * "AHB".index(side)
+        for k in ks:
+            dma(q, T.osc[4 * k:4 * k + 4, c:c + 128], T.fin_s[32 * k:32 * k + 4, c:c + 128], "sto", ["%ss%d" % (side, R)], [])
 
     for b in range(4):
         decode_own(0, b, True)
     for t in range(R):
-        wh, qp = "winH%d" % t, "qp%d" % t
+        wh, qp, xq = "winH%d" % t, "qp%d" % t, "xq%d" % t
         state_first(t)
         state_second(t)
         for b in range(3):
             decode_own(t, b, False)
         q_mx("dq", 0, 128, T.dr[:], ["dr0", "dr1", "dr2", "dr3"], ["dq"])
-        mm(0, "uq", 0, "dq", 0, True, True, ["uq", "dq"])
+        if t == 0:
+            late_constants()
+        beside(t, "A")
         mm(1, "dq", 0, "uq", 0, True, True, ["uq", "dq"])
+        mm(0, "uq", 0, "dq", 0, True, True, ["uq", "dq"])
         for b in range(4):
             if b == 3:
                 decode_own(t, b, False)
@@ -268,74 +295,88 @@ def rank_program(g, core, T, topo):
            ["ps1"], ["ac"])
         act(T.absS[:], bank(0), AF.Abs, ["ps0"], ["absS"])
         act(T.sgn[:], T.absS[:], AF.Sign, ["absS", "ac"], ["sgn", "lg"], scale=-1.0, bias=T.ac[:], accum_out=T.lg[:])
+        if t == 0:
+            late_tiles()
+        beside(t, "B")
         ts(T.eq[:, 1:129], T.absS[:], T.ac[:], -1.0, ["absS", "ac"], ["eq"], OP.is_equal, OP.mult)
         op("v", lambda e: e.tensor_tensor_scan(T.yy[:, 0:129], T.flip[:, 0:129], T.eq[:, 0:129], T.lg[:], OP.mult, OP.add),
            ["flip", "eq0", "eq", "lg"], ["yy"])
         y = T.yy[:, 128:129]
         for b in range(4):
             act(T.pt[:, b:512:4], bank(4 + b), AF.Copy, ["ps%d" % (4 + b)], ["pt%d" % b])
-        ts(T.xt[:], T.kk[:], y, None, ["kk0", "kk1", "kk2", "kk3", "yy"], ["xt"], OP.is_equal)
-        ts(T.pt[:, 512:544:4], T.below[:], y, y, ["below", "yy"], ["sl0"], OP.is_gt, OP.mult)
-        q_mx("xq", 0, 128, T.xt[:], ["xt"], ["xq"])
-        mm(2, "xq", 0, "wcq", 2, True, True, ["wcq", "xq"])
-        ts(T.pt[:, 513:544:2], T.above[:], y, None, ["above", "yy"], ["sl1"], OP.is_le)
-        q_mx(qp, 0, 136, T.pt[:], ["pt0", "pt1", "pt2", "pt3", "sl0", "sl1"], [qp])
-        mm(3, "wcq", 0, qp, 8, True, True, ["wcq", qp])
-        cp(T.offE[:, 4 * t:4 * t + 2], bank(2, 126, 128), ["ps2"], ["offE%d" % t])
-        pick(wh, NEW, K + 16, qp, 136, T.offE[:, 4 * t:4 * t + 3], ["offE%d" % t, "offS"], [qp], [qp],
+        for c in range(2):
+            ts(T.xt[:, c:512:4], T.kk[:, 128 * c:128 * c + 128], y, None, ["kk%d" % c, "yy"], ["xt%d" % c], OP.is_equal)
+        ts(T.xt[:, 512:512 + 4 * NS:2], T.below[:], y, y, ["below", "yy"], ["wrA"], OP.is_gt, OP.mult)
+        ts(T.xt[:, 513:512 + 4 * NS:2], T.below[:], y, float(NEW + K // 2), ["below", "yy"], ["wrB"], OP.is_gt, OP.mult)
+        q_mx(xq, 0, XW, T.xt[:], ["xt0", "xt1", "xt2", "wrA", "wrB"], [xq])
+        mm(2, xq, 0, "wcq", 6, True, True, ["wcq", xq])
+        sums(t, "H", 3)
+        q_mx(qp, 0, 128, T.pt[:], ["pt0", "pt1", "pt2", "pt3"], [qp])
+
+        def choice(out, c, key):
+            ts(out, bank(2, 124 + c, 125 + c), bank(2, 126 + c, 127 + c), None, ["ps2"], ["%s%d%d" % (key, c, t)], OP.add)
+
+        for c in range(2):
+            choice(T.offE[:, 2 * t + c:2 * t + c + 1], c, "offE")
+        pick(wh, NEW, K, qp, 128, T.offE[:, 2 * t:2 * t + 2], ["offE0%d" % t, "offE1%d" % t], [qp], [qp],
              ["newH%d" % t], ["newHs%d" % t])
 
-        def send(kind, view):
+        def send(kind, to, parts):
             tr = []
             for dst, side in ((right, "A"), (left, "B")):
                 rid, pid = topo.addr(dst)[:2]
-                tr.append(RemoteDMATransfer(dst_ids=[DstId(rid=rid, pnc=pid)], dma_engine_mask=sum(1 << e for e in masks[dst]),
-                                            remote_sem=T.sem["%s%s%d" % (kind, side, t)],
-                                            src=view(wh), dst=view("win%s%d" % (side, t))))
+                pairs = parts("%s%s%d" % (to, side, t))
+                w = len(masks[dst]) // len(pairs)
+                for i, (src, out) in enumerate(pairs):
+                    tr.append(RemoteDMATransfer(dst_ids=[DstId(rid=rid, pnc=pid)],
+                                                dma_engine_mask=sum(1 << e for e in masks[dst][w * i:w * i + w]),
+                                                remote_sem=T.sem["%s%s%d" % (kind, side, t)], src=src, dst=out))
             g.remote_dma_fused(tr, local_sem=T.sem.sent)
 
-        depend("g", ["newH%d" % t], [])
-        send("c", lambda name: T[name][:, NEW:END].bitcast(dt.uint8))
-        depend("g", ["newHs%d" % t], [])
-        send("s", lambda name: T[name + "_s"][:, NEW:END])
+        def codes(name, a, b):
+            return T[name][:, a:b].bitcast(dt.uint8)
 
-        renew(t, "H", 3)
-        cp(T.ech[:, 2 * t:2 * t + 2], bank(2, 126, 128), ["ps2"], ["ech%d" % t])
+        depend("g", [xq], [])
+        send("o", "sl", lambda w: [(codes(xq, P, P + NS), codes(w, P, P + NS)), (T[xq + "_s"][:, P:XW], T[w + "_s"][:, P:XW])])
+        depend("g", ["newH%d" % t], [])
+        send("c", "win", lambda w: [(codes(wh, NEW, END), codes(w, NEW, END))])
+        depend("g", ["newHs%d" % t], [])
+        send("s", "win", lambda w: [(T[wh + "_s"][:, NEW:END], T[w + "_s"][:, NEW:END])])
+
+        make_list(t, "H", 3)
+        renew(t, "H")
+        for c in range(2):
+            choice(T.ech[:, 2 * t + c:2 * t + c + 1], c, "ech")
         if t == 0:
             q_mx("wq", 0, 128, T.wb[:], ["wb"], ["wq"])
-        if t == R - 1:
-            g.sync.wait_ge(T.sem.sent, sent)
-        for q in range(2):
-            dma("y", T.ch[t:t + 1, 16 * q:16 * q + 16], T.ech[0:16, 2 * t + q:2 * t + q + 1], "sto", ["ech%d" % t], [])
+        for i, s in enumerate(order):
+            lands("sl%s%d" % (s, t), "o%s%d" % (s, t), arrives(left if s == "A" else right))
+            sums(t, s, i)
         if t < R - 1:
             for b in range(4):
                 decode_own(t + 1, b, True)
         else:
-            store("H", "y")
+            g.sync.wait_ge(T.sem.sent, sent)
+        for c in range(2):
+            dma("y", T.ch[t:t + 1, 16 * c:16 * c + 16], T.ech[0:16, 2 * t + c:2 * t + c + 1], "sto", ["ech%d%d" % (c, t)], [])
+        if t == R - 1:
+            store_codes("H")
+            store_scales("H", "y", range(4))
             dma("y", T.xe[:], T.xef[:], "sto", ["xef%d" % b for b in range(4)], [])
-            mm(0, "wq", 0, "winA%d" % t, 0, True, True, ["wq"] + both("A", t))
-            act(T.ysb[:, 0:P], bank(0), AF.Copy, ["ps0"], ["ysb0"])
 
         for i, s in enumerate(order):
             src = left if s == "A" else right
             lands("new%s%d" % (s, t), "c%s%d" % (s, t), arrives(src))
             lands("new%ss%d" % (s, t), "s%s%d" % (s, t), arrives(src))
-            new = ["new%s%d" % (s, t), "new%ss%d" % (s, t)] + both(s, t)
-            mm(2 + i, "wcq", 0, "win%s%d" % (s, t), END - 128, True, True, ["wcq"] + new)
-            if t == R - 1 and s == "A":
-                mm(1, "wq", 0, "winA%d" % t, END - 128, True, True, ["wq"] + new)
-        for i, s in enumerate(order):
-            if t == R - 1 and s == "A":
-                act(T.ysb[:, P:P + K], bank(1, 88, 120), AF.Copy, ["ps1"], ["ysb1"])
-            renew(t, s, 2 + i)
-            if t == R - 1 and s == "A":
-                (off0, key), (off1, key) = list_of(t, s, 0, 4), list_of(t, s, 4, 8)
-                cp(T.yp[:, 0:64], T.ysb[:].indirect(off0), ["ysb0", "ysb1", key], ["yp0"])
-                act(T.yp[:, 64:P], T.ysb[:].indirect(off1), AF.Copy, ["ysb0", "ysb1", key], ["yp1"])
-            if t == R - 1:
-                store(s, "sy")
-                if s == "A":
-                    dma("y", T.y[:], T.yp[:], "sto", ["yp0", "yp1"], [])
+            make_list(t, s, i)
+            renew(t, s)
 
+    mm(2, "wq", 0, "fin", 0, True, True, ["wq"] + both("A", R))
+    cp(T.yp[:], bank(2), ["ps2"], ["yp"])
+    for s in order:
+        store_codes(s)
+        store_scales(s, "y", (0, 2))
+        store_scales(s, "s", (1, 3))
+    dma("y", T.y[:], T.yp[:], "sto", ["yp"], [])
     finish()
     g.wait_ge(T.sem.sent, sent)

from concourse.bass import DstId, RemoteDMATransfer
from concourse.mybir import dt, AluOpType as OP, AxisListType, ActivationFunctionType as AF

P, K, R = 128, 32, 3
NEW, END = P, P + K
ROOM = 16
NS = ROOM // 4
XW = P + ROOM
CODE, BF, F32, U8, I32 = "float8_e4m3fn_x4", "bfloat16", "float32", "uint8", "int32"
FAR = 1024.0
ZW = 520

SCRATCH = {"ps": ("psum", [128, 4096], F32)}
for _n, _w, _d in (("hlb", 512, BF), ("hcb", 512, BF), ("hrb", 512, BF), ("xs", 512, BF), ("wb", 512, BF), ("ub4", 4, BF),
                   ("ubt", 512, BF), ("dr", 512, BF), ("pt", 512, BF), ("xt", 4 * XW, BF), ("ones", 136, BF),
                   ("idm", 128, BF), ("flip", 136, BF), ("zd", 3 * ZW, BF), ("wc", 4 * 134, BF), ("kk", 256, BF),
                   ("row16", 128, BF), ("pc", 4, I32), ("lo", 2, I32), ("hi", 2, I32), ("c16", 8, F32), ("pnum", 8, F32),
                   ("m1", 8, BF), ("m2", 8, BF), ("below", 8, BF), ("absS", 128, F32), ("ac", 1, F32),
                   ("sgn", 128, BF), ("lg", 1, F32), ("eq", 136, BF), ("yy", 136, BF), ("offE", 2 * R, "uint16"),
                   ("lst", 24, F32), ("offL", 24 * R, "uint16"), ("ech", 2 * R, F32), ("xef", 512, F32), ("yp", 128, F32)):
    SCRATCH[_n] = ("sbuf", [128, _w], _d)
for _n, _w in [("e1", 512), ("e25", 512), ("em5", 512), ("wcq", 134), ("ws1", 128), ("uq", 128), ("wq", 128), ("dq", 128),
               ("fin", 384)] + [("%s%d" % (_a, _t), _b) for _t in range(R) for _a, _b in (
                   ("winA", END), ("winB", END), ("winH", END), ("qp", 128), ("xq", XW), ("slA", XW), ("slB", XW))]:
    SCRATCH[_n] = ("sbuf", [128, _w], CODE)
    SCRATCH[_n + "_s"] = ("sbuf", [128, _w], U8)

SEMAPHORES = ["sv", "ss", "sp", "sg", "sent", "sto"] + ["ld" + n for n in ("hl", "hc", "hr", "x", "w", "u")] + [
    "%s%s%d" % (k, s, t) for k in "ocs" for s in "AB" for t in range(R)]


def _flow(g, T):
    eng = {"v": g.vector, "s": g.scalar, "p": g.tensor, "g": g, "y": g.sync}
    own = {"v": "sv", "s": "ss", "p": "sp", "g": "sg"}
    known = {q: {} for q in eng}
    total, clock, lastw, reads = {}, {}, {}, {}

    def wait(q, events):
        need = {}
        for s, n in events:
            if known[q].get(s, 0) < n and need.get(s, 0) < n:
                need[s] = n
        for s in sorted(need):
            if not any(s2 != s and clock[(s2, n2)].get(s, 0) >= need[s] for s2, n2 in need.items()):
                eng[q].wait_ge(T.sem[s], need[s])
        for s, n in need.items():
            for k, c in clock[(s, n)].items():
                known[q][k] = max(known[q].get(k, 0), c)

    def depend(q, rd, wr):
        ev = []
        for k in list(rd) + list(wr):
            bank = k.startswith("ps")
            if k in lastw and not (bank and q == "p" and lastw[k][0] == "p"):
                ev.append(lastw[k][1])
            if bank or k in wr:
                ev += [e for q2, e in reads.get(k, ()) if q2 != q or k in wr]
        wait(q, ev)

    def done(q, who, sem, inc, rd, wr):
        total[sem] = total.get(sem, 0) + inc
        event = (sem, total[sem])
        clock[event] = dict(known[q])
        clock[event][sem] = total[sem]
        for k in rd:
            reads.setdefault(k, []).append((who, event))
        for k in wr:
            lastw[k] = (who, event)
            reads[k] = []

    def op(q, fn, rd, wr):
        depend(q, rd, wr)
        fn(eng[q]).then_inc(T.sem[own[q]], 1)
        done(q, q, own[q], 1, rd, wr)

    def dma(q, out, in_, sem, rd, wr):
        depend(q, rd, wr)
        eng[q].dma_start(out, in_).then_inc(T.sem[sem], 16)
        done(q, "d" + q, sem, 16, rd, wr)

    def lands(key, sem, n):
        total[sem] = n
        clock[(sem, n)] = {sem: n}
        lastw[key] = ("r", (sem, n))

    def finish():
        for s in sorted(total):
            if known["g"].get(s, 0) < total[s]:
                g.wait_ge(T.sem[s], total[s])

    return op, dma, depend, lands, finish


def _masks(topo, core, left, right):
    taken, out = set(), {}
    for dst in sorted((left, right), key=lambda c: len(topo.engines(core, c))):
        out[dst] = [k for k in topo.engines(core, dst) if k not in taken][:8]
        taken.update(out[dst])
    return out


def rank_program(g, core, T, topo):
    rank = T.rank_of(core)
    if rank is None:
        return
    cores = list(T.cores)
    n = len(cores)
    left, right = cores[(rank - 1) % n], cores[(rank + 1) % n]
    masks = _masks(topo, core, left, right)
    sent = 3 * R * sum(len(m) for m in masks.values())

    def arrives(src):
        k = cores.index(src)
        return len(_masks(topo, src, cores[(k - 1) % n], cores[(k + 1) % n])[core])

    op, dma, depend, lands, finish = _flow(g, T)
    ps = T["ps"]

    def bank(b, lo=0, hi=128):
        return ps[:, 512 * b + lo:512 * b + hi]

    def q_mx(name, a, b, tile, rd, wr):
        op("v", lambda e: e.quantize_mx(T[name][:, a:b], T[name + "_s"][:, a:b], tile), rd, wr)

    def mm(b, ln, la, rn, ra, start, stop, rd, w=128):
        op("p", lambda e: e.matmul_mx(bank(b, 0, w), T[ln][:, la:la + 128], T[ln + "_s"][:, la:la + 128],
                                      T[rn][:, ra:ra + w], T[rn + "_s"][:, ra:ra + w], start, stop),
           rd, ["ps%d" % b])

    def act(out, in_, func, rd, wr, **kw):
        op("s", lambda e: e.activation(out, in_, func, **kw), rd, wr)

    def ts(out, in_, s1, s2, rd, wr, *ops):
        op("v", lambda e: e.tensor_scalar(out, in_, s1, s2, *ops), rd, wr)

    def tt(out, a, b, o, rd, wr):
        op("v", lambda e: e.tensor_tensor(out, a, b, o), rd, wr)

    def cp(out, in_, rd, wr):
        op("v", lambda e: e.tensor_copy(out, in_), rd, wr)

    def fill(ap, c, wr):
        op("v", lambda e: e.memset(ap, c), [], wr)

    def iota(out, pattern, base, cm, wr, **kw):
        op("g", lambda e: e.iota(out, pattern, base, cm, **kw), [], wr)

    def choose(out, in_, pattern, cond, other, base, cm, rd, wr):
        op("g", lambda e: e.affine_select(out, in_, pattern, cond, other, base, cm), rd, wr)

    order = ["A", "B"]
    if topo.chip(left) != topo.chip(core) and topo.chip(right) == topo.chip(core):
        order = ["B", "A"]
    first = {"A": "hl", "B": "hr"}

    dma("s", T.hcb[:], T.hc[:], "ldhc", [], ["hcb"])
    dma("y", T[first[order[0]] + "b"][:], T[first[order[0]]][:], "ld" + first[order[0]], [], [first[order[0]] + "b"])
    dma("s", T[first[order[1]] + "b"][:], T[first[order[1]]][:], "ld" + first[order[1]], [], [first[order[1]] + "b"])
    dma("y", T.ub4[:], T.u[:, 0:4], "ldu", [], ["ub4"])
    dma("y", T.xs[:], T.x[:], "ldx", [], ["xs0", "xs1", "xs2", "xs3"])
    dma("y", T.wb[:], T.w[:], "ldw", [], ["wb"])

    small = {"allow_small_or_imprecise_dtypes": True}
    fill(T.ones[:], 1.0, ["ones"])
    for f in range(3):
        fill(T.zd[:, ZW * f:ZW * f + ZW], 0.0, ["zd%d" % f])
    choose(T.idm[:], T.ones[:, 0:128], [[-1, 128]], OP.is_equal, 0.0, 0, 1, ["ones"], ["idm"])
    iota(T.pc[:], [[0, 4]], 0, 1, ["pc"])
    iota(T.row16[:], [[0, 8], [1, 16]], 0, 0, ["row16"], **small)
    for c in range(2):
        iota(T.kk[:, 128 * c:128 * c + 128], [[0, 8], [2, 16]], K * (c - 1), 0, ["kk%d" % c], **small)
    choose(T.m1[:], T.ones[:, 0:8], [[-16, NS], [-16 * NS, 2]], OP.is_ge, 0.0, 0, 1, ["ones"], ["m1"])
    choose(T.m2[:], T.m1[:], [[16, NS], [16 * NS, 2]], OP.is_ge, 0.0, 15, -1, ["m1"], ["m2"])
    choose(T.flip[:], T.ones[:], [[-1, 136]], OP.not_equal, -1.0, 1, 1, ["ones"], ["flip"])
    iota(T.c16[:], [[16, 8]], 0, 0, ["c16"], **small)
    cp(T.zd[:, 3:515:4], T.idm[:], ["idm"], ["zd0"])
    for f, s in ((1, 0.25), (2, -0.5)):
        act(T.zd[:, ZW * f + 3:ZW * f + 515:4], T.idm[:], AF.Copy, ["idm"], ["zd%d" % f], scale=s)
    for t in range(4):
        act(T.ubt[:, t:512:4], T.ones[:, 0:128], AF.Identity, ["ones", "ub4"], ["ubt%d" % t], scale=0.0, bias=T.ub4[:, t:t + 1])
    act(T.below[:], T.m2[:], AF.Identity, ["m2"], ["below"], scale=FAR + K, bias=-FAR)

    low = T.wc[:, 520:521]

    def decoders(f, name):
        for b in range(4):
            q_mx(name, 128 * b, 128 * b + 128, T.zd[:, ZW * f + 3 - b:ZW * f + 515 - b], ["zd%d" % f], ["%s%d" % (name, b)])

    decoders(0, "e1")
    q_mx("winH0", 0, 128, T.hcb[:], ["hcb"], ["H0", "Hs0"])
    decoders(1, "e25")
    for s in order:
        q_mx("win%s0" % s, 0, 128, T[first[s] + "b"][:], [first[s] + "b"], ["%s0" % s, "%ss0" % s])
        if s == order[0]:
            fill(T.wc[:], 0.0, ["wcc", "wcw0", "wcw1"])
            fill(T.xt[:], 0.0, ["xt0", "xt1", "xt2", "wrA", "wrB"])
            fill(T.eq[:, 0:1], -float(P - K), ["eq0"])
            ts(T.lo[:], T.pc[:, 0:2], 15, None, ["pc"], ["lo"], OP.bitwise_and)
            ts(T.hi[:], T.pc[:, 0:2], 112, None, ["pc"], ["hi"], OP.bitwise_and)
            cp(T.wc[:, 520:526:5], T.lo[:], ["lo"], ["wcc"])
            cp(T.wc[:, 528:534:5], T.hi[:], ["hi"], ["wcc"])
    decoders(2, "em5")
    q_mx("uq", 0, 128, T.ubt[:], ["ubt0", "ubt1", "ubt2", "ubt3"], ["uq"])

    def late_constants():
        ts(T.wc[:, 2:512:4], T.row16[:], low, 0.5, ["row16", "wcc"], ["wcw0"], OP.is_equal, OP.mult)
        ts(T.wc[:, 3:512:4], T.row16[:], low, None, ["row16", "wcc"], ["wcw1"], OP.is_equal)
        act(T.pnum[:], T.c16[:], AF.Identity, ["c16", "wcc"], ["pnum"], bias=low)

    def late_tiles():
        q_mx("wcq", 0, 134, T.wc[:], ["wcw0", "wcw1", "wcc"], ["wcq"])
        q_mx("ws1", 0, 128, T.wc[:, 2:514], ["wcw0", "wcw1", "wcc"], ["ws1"])

    def both(side, t):
        return ["%s%d" % (side, t), "%ss%d" % (side, t)]

    def state_first(t):
        for b in range(4):
            mm(b, "e25", 128 * b, "win%s%d" % (order[0], t), 0, True, False, ["e25%d" % b] + both(order[0], t))

    def state_second(t):
        for b in range(4):
            mm(b, "e25", 128 * b, "win%s%d" % (order[1], t), 0, False, False, ["e25%d" % b] + both(order[1], t))
            mm(b, "em5", 128 * b, "winH%d" % t, 0, False, True, ["em5%d" % b] + both("H", t))
            xb = T.xs[:, b:512:4]
            tt(xb, xb, bank(b), OP.add, ["xs%d" % b, "ps%d" % b], ["xs%d" % b])
            if t == R - 1:
                act(T.xef[:, b:512:4], xb, AF.Copy, ["xs%d" % b], ["xef%d" % b])
            for k in ([b - 1] if b else []) + ([b] if b == 3 else []):
                tt(T.dr[:, k:512:4], T.xs[:, k:512:4], bank(4 + k), OP.subtract, ["xs%d" % k, "ps%d" % (4 + k)], ["dr%d" % k])

    def decode_own(t, b, alone):
        mm(4 + b, "e1", 128 * b, "winH%d" % t, 0, True, alone, ["e1%d" % b] + both("H", t))

    def pick(dst, c, w, src, hi, off, keys, rd, rds, wr, wrs):
        cp(T[dst][:, c:c + w].bitcast(dt.uint32), T[src][:, 0:hi].bitcast(dt.uint32).indirect(off), keys + rd, wr)
        act(T[dst + "_s"][:, c:c + w], T[src + "_s"][:, 0:hi].indirect(off), AF.Copy, keys + rds, wrs)

    def list_of(t, side):
        k = 24 * t + 8 * "HAB".index(side)
        return T.offL[:, k:k + 8], "off%s%d" % (side, t)

    def beside(t, side):
        name = "sl%s%d" % (side, t)
        q_mx(name, 0, P, T.dr[:], ["dr0", "dr1", "dr2", "dr3"], ["by" + name])

    def sums(t, side, b):
        name = "xq%d" % t if side == "H" else "sl%s%d" % (side, t)
        rd = [name] if side == "H" else [name, "by" + name]
        mm(b, "wcq", 0, name, 0, True, True, ["wcq"] + rd, P + NS)
        mm(b, "ws1", 0, name, NS, True, True, ["ws1"] + rd)

    def make_list(t, side, b):
        off, key = list_of(t, side)
        k = 8 * "HAB".index(side)
        f = T.lst[:, k:k + 8]
        tt(f, bank(b, P - NS, P + NS), T.pnum[:], OP.max, ["ps%d" % b, "pnum"], ["lst" + side])
        cp(off, f, ["lst" + side], [key])

    def renew(t, side):
        off, key = list_of(t, side)
        dst, c = ("win%s%d" % (side, t + 1), 0) if t < R - 1 else ("fin", 128 * "AHB".index(side))
        pick(dst, c, P, "win%s%d" % (side, t), END, off, [key],
             ["%s%d" % (side, t), "new%s%d" % (side, t)], ["%ss%d" % (side, t), "new%ss%d" % (side, t)],
             ["%s%d" % (side, t + 1)], ["%ss%d" % (side, t + 1)])

    def store_codes(side):
        c = 128 * "AHB".index(side)
        dma("y", T.oc[:, 4 * c:4 * c + 512], T.fin[:, c:c + 128].bitcast(dt.uint8), "sto", ["%s%d" % (side, R)], [])

    def store_scales(side, q, ks):
        c = 128 * "AHB".index(side)
        for k in ks:
            dma(q, T.osc[4 * k:4 * k + 4, c:c + 128], T.fin_s[32 * k:32 * k + 4, c:c + 128], "sto", ["%ss%d" % (side, R)], [])

    for b in range(4):
        decode_own(0, b, True)
    for t in range(R):
        wh, qp, xq = "winH%d" % t, "qp%d" % t, "xq%d" % t
        state_first(t)
        state_second(t)
        for b in range(3):
            decode_own(t, b, False)
        q_mx("dq", 0, 128, T.dr[:], ["dr0", "dr1", "dr2", "dr3"], ["dq"])
        if t == 0:
            late_constants()
        beside(t, "A")
        mm(1, "dq", 0, "uq", 0, True, True, ["uq", "dq"])
        mm(0, "uq", 0, "dq", 0, True, True, ["uq", "dq"])
        for b in range(4):
            if b == 3:
                decode_own(t, b, False)
            mm(4 + b, "e1", 128 * b, "dq", 0, False, True, ["e1%d" % b, "dq"])
        op("v", lambda e: e.tensor_reduce(T.ac[:], bank(1, 0, 1), AxisListType.X, OP.max, apply_absolute_value=True),
           ["ps1"], ["ac"])
        act(T.absS[:], bank(0), AF.Abs, ["ps0"], ["absS"])
        act(T.sgn[:], T.absS[:], AF.Sign, ["absS", "ac"], ["sgn", "lg"], scale=-1.0, bias=T.ac[:], accum_out=T.lg[:])
        if t == 0:
            late_tiles()
        beside(t, "B")
        ts(T.eq[:, 1:129], T.absS[:], T.ac[:], -1.0, ["absS", "ac"], ["eq"], OP.is_equal, OP.mult)
        op("v", lambda e: e.tensor_tensor_scan(T.yy[:, 0:129], T.flip[:, 0:129], T.eq[:, 0:129], T.lg[:], OP.mult, OP.add),
           ["flip", "eq0", "eq", "lg"], ["yy"])
        y = T.yy[:, 128:129]
        for b in range(4):
            act(T.pt[:, b:512:4], bank(4 + b), AF.Copy, ["ps%d" % (4 + b)], ["pt%d" % b])
        for c in range(2):
            ts(T.xt[:, c:512:4], T.kk[:, 128 * c:128 * c + 128], y, None, ["kk%d" % c, "yy"], ["xt%d" % c], OP.is_equal)
        ts(T.xt[:, 512:512 + 4 * NS:2], T.below[:], y, y, ["below", "yy"], ["wrA"], OP.is_gt, OP.mult)
        ts(T.xt[:, 513:512 + 4 * NS:2], T.below[:], y, float(NEW + K // 2), ["below", "yy"], ["wrB"], OP.is_gt, OP.mult)
        q_mx(xq, 0, XW, T.xt[:], ["xt0", "xt1", "xt2", "wrA", "wrB"], [xq])
        mm(2, xq, 0, "wcq", 6, True, True, ["wcq", xq])
        sums(t, "H", 3)
        q_mx(qp, 0, 128, T.pt[:], ["pt0", "pt1", "pt2", "pt3"], [qp])

        def choice(out, c, key):
            ts(out, bank(2, 124 + c, 125 + c), bank(2, 126 + c, 127 + c), None, ["ps2"], ["%s%d%d" % (key, c, t)], OP.add)

        for c in range(2):
            choice(T.offE[:, 2 * t + c:2 * t + c + 1], c, "offE")
        pick(wh, NEW, K, qp, 128, T.offE[:, 2 * t:2 * t + 2], ["offE0%d" % t, "offE1%d" % t], [qp], [qp],
             ["newH%d" % t], ["newHs%d" % t])

        def send(kind, to, parts):
            tr = []
            for dst, side in ((right, "A"), (left, "B")):
                rid, pid = topo.addr(dst)[:2]
                pairs = parts("%s%s%d" % (to, side, t))
                w = len(masks[dst]) // len(pairs)
                for i, (src, out) in enumerate(pairs):
                    tr.append(RemoteDMATransfer(dst_ids=[DstId(rid=rid, pnc=pid)],
                                                dma_engine_mask=sum(1 << e for e in masks[dst][w * i:w * i + w]),
                                                remote_sem=T.sem["%s%s%d" % (kind, side, t)], src=src, dst=out))
            g.remote_dma_fused(tr, local_sem=T.sem.sent)

        def codes(name, a, b):
            return T[name][:, a:b].bitcast(dt.uint8)

        depend("g", [xq], [])
        send("o", "sl", lambda w: [(codes(xq, P, P + NS), codes(w, P, P + NS)), (T[xq + "_s"][:, P:XW], T[w + "_s"][:, P:XW])])
        depend("g", ["newH%d" % t], [])
        send("c", "win", lambda w: [(codes(wh, NEW, END), codes(w, NEW, END))])
        depend("g", ["newHs%d" % t], [])
        send("s", "win", lambda w: [(T[wh + "_s"][:, NEW:END], T[w + "_s"][:, NEW:END])])

        make_list(t, "H", 3)
        renew(t, "H")
        for c in range(2):
            choice(T.ech[:, 2 * t + c:2 * t + c + 1], c, "ech")
        if t == 0:
            q_mx("wq", 0, 128, T.wb[:], ["wb"], ["wq"])
        for i, s in enumerate(order):
            lands("sl%s%d" % (s, t), "o%s%d" % (s, t), arrives(left if s == "A" else right))
            sums(t, s, i)
        if t < R - 1:
            for b in range(4):
                decode_own(t + 1, b, True)
        else:
            g.sync.wait_ge(T.sem.sent, sent)
        for c in range(2):
            dma("y", T.ch[t:t + 1, 16 * c:16 * c + 16], T.ech[0:16, 2 * t + c:2 * t + c + 1], "sto", ["ech%d%d" % (c, t)], [])
        if t == R - 1:
            store_codes("H")
            store_scales("H", "y", range(4))
            dma("y", T.xe[:], T.xef[:], "sto", ["xef%d" % b for b in range(4)], [])

        for i, s in enumerate(order):
            src = left if s == "A" else right
            lands("new%s%d" % (s, t), "c%s%d" % (s, t), arrives(src))
            lands("new%ss%d" % (s, t), "s%s%d" % (s, t), arrives(src))
            make_list(t, s, i)
            renew(t, s)

    mm(2, "wq", 0, "fin", 0, True, True, ["wq"] + both("A", R))
    cp(T.yp[:], bank(2), ["ps2"], ["yp"])
    for s in order:
        store_codes(s)
        store_scales(s, "y", (0, 2))
        store_scales(s, "s", (1, 3))
    dma("y", T.y[:], T.yp[:], "sto", ["yp"], [])
    finish()
    g.wait_ge(T.sem.sent, sent)
